import numpy as np
import ml_dtypes


def mxq(x, axis, fmt="e4m3"):
    dtype, down = {"e4m3": (ml_dtypes.float8_e4m3fn, 7), "e5m2": (ml_dtypes.float8_e5m2, 14)}[fmt]
    v = np.moveaxis(np.asarray(x, np.float32).astype(ml_dtypes.bfloat16).astype(np.float64), axis, -1)
    blocks = v.reshape(v.shape[:-1] + (-1, 32))
    amax = np.abs(blocks).max(-1, keepdims=True)
    byte = np.maximum(np.where(amax > 0, np.frexp(amax)[1] - 1 + 127, 0) - down, 1)
    scale = np.exp2(byte - 127.0)
    codes = (blocks / scale).astype(np.float32).astype(dtype).astype(np.float64)
    return np.moveaxis((codes * scale).reshape(v.shape), -1, axis)


WIDE = False


def mx_kscale(k):
    if not WIDE:
        return np.ones(k)
    levels = np.array([10, -10, 5, -5, 0])
    if k % 512:
        return np.exp2(np.random.permutation(np.resize(levels, k // 32))).repeat(32)
    a = np.empty((k // 512, 16))
    for p in range(k // 512):
        a[p, :8] = np.random.permutation(np.resize(levels, 8))
        for g in range(8):
            far = levels[np.abs(levels - a[p, g]) >= 10]
            a[p, g + 8] = far[np.random.randint(len(far))]
    return np.exp2(a.ravel()).repeat(32)


def f64(x):
    return np.asarray(x).astype(np.float64)


def striped(idx):
    return np.tile(idx.reshape(-1, 16).T, (8, 1)).astype(np.uint16)


def unstriped(offs):
    return offs[:16].T.reshape(-1).astype(np.int64)


E2M1 = np.array([0.0, 0.5, 1.0, 1.5, 2.0, 3.0, 4.0, 6.0, -0.0, -0.5, -1.0, -1.5, -2.0, -3.0, -4.0, -6.0])


def pack_weight(w, fmt):
    k, n = w.shape
    w = f64(np.asarray(w, np.float32).astype(ml_dtypes.bfloat16)).reshape(k // 32, 32, n)
    amax = np.abs(w).max(1)
    if fmt == "e4m3":
        byte = np.frexp(amax)[1] - 1 + 127 - 7
    else:
        mant, ex = np.frexp(amax / 6.0)
        byte = np.where(mant > 0.5, ex, ex - 1) + 127
    byte = np.clip(np.where(amax > 0, byte, 1), 1, 254)
    scaled = (w * np.exp2(127.0 - byte)[:, None, :]).reshape(k, n).astype(np.float32)
    by_word = np.ascontiguousarray(scaled.reshape(k // 512, 128, 4, n).transpose(0, 1, 3, 2))
    if fmt == "e4m3":
        words = by_word.astype(ml_dtypes.float8_e4m3fn).view(np.uint8)
    else:
        c = by_word.astype(ml_dtypes.float4_e2m1fn).view(np.uint8) & 0xF
        words = (c[..., 0::2] | (c[..., 1::2] << 4)).reshape(k // 512, 128, 2 * n)
    return np.ascontiguousarray(words), np.ascontiguousarray(byte.astype(np.uint8).reshape(k // 512, 16, n))


def unpack_weight(words, scales, fmt):
    g, _, n = scales.shape
    words = np.ascontiguousarray(words).reshape(g, 128, n, -1)
    if fmt == "e4m3":
        vals = words.view(ml_dtypes.float8_e4m3fn).astype(np.float64)
    else:
        nib = np.empty((g, 128, n, 4), np.uint8)
        nib[..., 0::2] = words & 0xF
        nib[..., 1::2] = words >> 4
        vals = E2M1[nib]
    vals = vals * np.repeat(np.exp2(scales.astype(np.float64) - 127.0), 8, axis=1)[..., None]
    return vals.transpose(0, 1, 3, 2).reshape(g * 512, n)


def gelu(v):
    return 0.5 * v * (1.0 + np.tanh(np.sqrt(2.0 / np.pi) * (v + 0.044715 * v**3)))


def bf(x):
    return np.asarray(x, np.float32).astype(ml_dtypes.bfloat16)

def planes(Y):
    n, m = Y.shape
    b = f64(bf(Y)).reshape(n // 32, 32, m)
    amax = np.abs(b).max(1)
    byte = np.clip(np.where(amax > 0, np.frexp(amax)[1] - 1 + 127 - 7, 1), 1, 254)
    codes = (b * np.exp2(127.0 - byte)[:, None, :]).reshape(n, m).astype(np.float32).astype(ml_dtypes.float8_e4m3fn).view(np.uint8)
    words = codes.reshape(n // 512, 128, 4, m).transpose(0, 1, 3, 2)
    return np.ascontiguousarray(words), np.ascontiguousarray(byte.astype(np.uint8).reshape(n // 512, 16, m))


K, T, S, H, N = 1024, 2048, 512, 1024, 512

def setup_inputs():
    n = np.random.standard_normal
    s = mx_kscale(K)[:, None]
    u = mx_kscale(H)[:, None]
    tab_words, tab_scales = pack_weight(n((K, T)) * s, "e4m3")
    wbus_words, wbus_scales = pack_weight(0.33 * n((K, H)) / np.sqrt(K) / s, "e2m1")
    wadj_words, wadj_scales = pack_weight(0.33 * n((K, H)) / np.sqrt(K) / s, "e4m3")
    wline = n((K, H)) / np.sqrt(K) / s * u.T
    wstate = 2.0 * n((H, N)) / np.sqrt(H) / u
    return {
        "tab_words": tab_words, "tab_scales": tab_scales,
        "wbus_words": wbus_words, "wbus_scales": wbus_scales,
        "wadj_words": wadj_words, "wadj_scales": wadj_scales,
        "wline": wline.astype(np.float32),
        "wstate": wstate.astype(np.float32),
        "pinj": (0.8 * n(N)).astype(np.float32),
        "minv": np.exp(0.8 * n(N)).astype(np.float32),
        "offs": striped(np.random.permutation(T)[:S]),
        "offs2": striped(np.random.permutation(T)[:S]),
        "offs3": striped(np.random.permutation(T)[:S]),
    }

def reference(tab_words, tab_scales, wbus_words, wbus_scales, wadj_words, wadj_scales, wline, wstate, pinj, minv, offs, offs2, offs3):
    v = unpack_weight(tab_words, tab_scales, "e4m3")[:, unstriped(offs)]
    va = unpack_weight(tab_words, tab_scales, "e4m3")[:, unstriped(offs2)]
    vl = unpack_weight(tab_words, tab_scales, "e4m3")[:, unstriped(offs3)]
    bus = unpack_weight(wbus_words, wbus_scales, "e2m1").T @ v
    adj = unpack_weight(wadj_words, wadj_scales, "e4m3").T @ va
    line = mxq(f64(wline), 0, "e4m3").T @ vl
    h = np.sin(bus - adj) * line
    flow = mxq(f64(wstate), 0, "e4m3").T @ mxq(h, 0, "e4m3")
    y = (f64(pinj)[:, None] - flow) * f64(minv)[:, None]
    words, scales = planes(y)
    return y, words, scales

@@ -1,0 +1,365 @@
+from contextlib import ExitStack
+
+import concourse.mybir as mybir
+from concourse.masks import make_identity
+
+K, T, S, H, N = 1024, 2048, 512, 1024, 512
+FLOPS = 2 * (3 * K * H * S + H * N * S)
+
+F32 = mybir.dt.float32
+BF16 = mybir.dt.bfloat16
+I32 = mybir.dt.int32
+U32 = mybir.dt.uint32
+U16 = mybir.dt.uint16
+U8 = mybir.dt.uint8
+FP8X4 = mybir.dt.float8_e4m3fn_x4
+FP4X4 = mybir.dt.float4_e2m1fn_x4
+ACT = mybir.ActivationFunctionType
+ALU = mybir.AluOpType
+
+P = 128
+PACK = 4
+KP = P * PACK
+QUADS = 4
+JT = S // P
+
+
+def tile_list_grid_swing_flow_kernel(
+    tc, tab_words, tab_scales, wbus_words, wbus_scales, wadj_words, wadj_scales,
+    wline, wstate, pinj, minv, offs, offs2, offs3, out_0, out_1, out_2,
+):
+    nc = tc.nc
+    with ExitStack() as ctx:
+        keep = ctx.enter_context(tc.tile_pool(name="keep", bufs=1))
+        ring = ctx.enter_context(tc.tile_pool(name="ring", bufs=3))
+        psum = ctx.enter_context(tc.psum_pool(name="psum", bufs=2))
+
+        def kept(shape, dtype, name):
+            return keep.tile(shape, dtype, name=name, align_bytes=64)
+
+        tab_sc = kept([P, T], U8, "tab_sc")
+        adj_sc = kept([P, H], U8, "adj_sc")
+        bus_sc = kept([P, 2, H], U8, "bus_sc")
+        v_sc_hi = kept([P, S], U8, "v_sc_hi")
+        warm = kept([P, 1], F32, "warm")
+        warm2 = kept([P, 1], F32, "warm2")
+        ident = kept([P, P], F32, "ident")
+        pin = kept([P, PACK], F32, "pin")
+        inv = kept([P, PACK], F32, "inv")
+        neg_inv = kept([P, PACK], F32, "neg_inv")
+        pin_inv = kept([P, PACK], F32, "pin_inv")
+        lists = {}
+        wl_raw, adj_w, bus_w, tab_w, ws_raw = {}, {}, {}, {}, {}
+        wl_bf, wl_q, ws_bf, ws_q, got, got_sc, sines, hs, h_q = {}, {}, {}, {}, {}, {}, {}, {}, {}
+
+        def load_list(name, src):
+            lists[name] = keep.tile([P, S // 16], U16, name="list_" + name)
+            nc.sync.dma_start(lists[name][:], src)
+
+        def tab_scales_in(eng):
+            for q in range(QUADS):
+                eng.dma_start(
+                    out=tab_sc[32 * q : 32 * q + 8, :].bitcast(I32),
+                    in_=tab_scales[:, 4 * q : 4 * q + 4, :].bitcast(I32),
+                )
+
+        def adj_scales_in(eng):
+            for q in range(QUADS):
+                eng.dma_start(
+                    out=adj_sc[32 * q : 32 * q + 8, :].bitcast(I32),
+                    in_=wadj_scales[:, 4 * q : 4 * q + 4, :].bitcast(I32),
+                )
+
+        def bus_scales_in(eng):
+            for q in range(QUADS):
+                eng.dma_start(
+                    out=bus_sc[32 * q : 32 * q + 4, :, :].bitcast(I32),
+                    in_=wbus_scales[:, 4 * q : 4 * q + 4, :].rearrange("a r c -> r a c").bitcast(I32),
+                )
+
+        def load_tab(a):
+            tab_w[a] = kept([P, T], U32, "tab_w%d" % a)
+            nc.sync.dma_start(out=tab_w[a][:].bitcast(I32), in_=tab_words[a].rearrange("p t i -> p (t i)").bitcast(I32))
+
+        def load_adj(c):
+            adj_w[c] = kept([P, 2, KP], U32, "adj_w%d" % c)
+            nc.sync.dma_start(
+                out=adj_w[c][:].bitcast(I32),
+                in_=wadj_words.rearrange("a p c i -> p a (c i)")[:, :, 4 * KP * c : 4 * KP * (c + 1)].bitcast(I32),
+            )
+
+        def load_bus(c):
+            bus_w[c] = kept([P, 2, 2 * KP], U8, "bus_w%d" % c)
+            nc.sync.dma_start(
+                out=bus_w[c][:].bitcast(I32),
+                in_=wbus_words.rearrange("a p c -> p a c")[:, :, 2 * KP * c : 2 * KP * (c + 1)].bitcast(I32),
+            )
+
+        def load_line(c, a):
+            wl_raw[c, a] = kept([P, PACK, KP], F32, "wl_raw%d%d" % (c, a))
+            rows = wline[KP * a : KP * (a + 1), KP * c : KP * (c + 1)]
+            nc.sync.dma_start(out=wl_raw[c, a][:], in_=rows.rearrange("(p i) c -> p i c", i=PACK))
+
+        def load_state(g):
+            ws_raw[g] = kept([P, PACK, N], F32, "ws_raw%d" % g)
+            rows = wstate[KP * g : KP * (g + 1), :].rearrange("(u t q) n -> t u q n", t=PACK, q=4)
+            for t in range(PACK):
+                nc.sync.dma_start(out=ws_raw[g][:, t, :], in_=rows[t])
+
+        def gather_scales(name):
+            got_sc[name] = kept([P, S], U8, "picked_sc_" + name)
+            nc.vector.tensor_copy(got_sc[name][:], tab_sc[:].indirect(lists[name][:]))
+
+        def gather_words(name, a):
+            got[name, a] = kept([P, S], U32, "%s_v%d" % (name, a))
+            nc.vector.tensor_copy(got[name, a][:], tab_w[a][:].indirect(lists[name][:]))
+
+        def round_line(c, a, *copies):
+            wl_bf[c, a] = kept([P, PACK, P, PACK], BF16, "wl_bf%d%d" % (c, a))
+            w = 32 // len(copies)
+            for n, copy in enumerate(copies):
+                copy(
+                    out=wl_bf[c, a][:].rearrange("p t (u q) i -> p u t i q", q=4)[:, w * n : w * (n + 1)],
+                    in_=wl_raw[c, a][:].rearrange("p i (u t q) -> p u t i q", t=PACK, q=4)[:, w * n : w * (n + 1)],
+                )
+
+        def round_state(g, *copies):
+            ws_bf[g] = kept([P, PACK, P, PACK], BF16, "ws_bf%d" % g)
+            w = P // len(copies)
+            for n, copy in enumerate(copies):
+                copy(
+                    out=ws_bf[g][:].rearrange("p t m i -> p m i t")[:, w * n : w * (n + 1)],
+                    in_=ws_raw[g][:].rearrange("p i (m t) -> p m i t", t=PACK)[:, w * n : w * (n + 1)],
+                )
+
+        def quantise(bf, name):
+            codes = kept([P, KP], U32, name + "_w")
+            sc = kept([P, KP], U8, name + "_s")
+            nc.vector.quantize_mx(out=codes[:].bitcast(FP8X4), scales=sc[:], in_=bf[:].rearrange("p t m i -> p (t m i)"))
+            return codes, sc
+
+        def quantise_line(c, a):
+            wl_q[c, a] = quantise(wl_bf[c, a], "wl_q%d%d" % (c, a))
+
+        def quantise_state(g):
+            ws_q[g] = quantise(ws_bf[g], "ws_q%d" % g)
+
+        adj_sb, diffs = {}, {}
+
+        def adjacent(c, jt):
+            js = slice(P * jt, P * (jt + 1))
+            adj = psum.tile([P, KP], F32, tag="acc", name="adj", bufs=4)
+            for a in range(2):
+                nc.tensor.matmul_mx(
+                    out=adj[:], lhsT=got["adj", a][:, js].bitcast(FP8X4), lhsT_scale=got_sc["adj"][4 * a :, js],
+                    rhs=adj_w[c][:, a, :].bitcast(FP8X4), rhs_scale=adj_sc[4 * a :, KP * c : KP * (c + 1)],
+                    start=(a == 0), stop=(a == 1),
+                )
+            adj_sb[c, jt] = ring.tile([P, PACK, P], F32, tag="adj_sb", name="adj_sb", bufs=8)
+            nc.scalar.copy(
+                out=adj_sb[c, jt][:].rearrange("j t (u q) -> j t u q", q=4),
+                in_=adj[:].rearrange("j (u t q) -> j t u q", t=PACK, q=4),
+            )
+
+        def angle(c, jt):
+            js = slice(P * jt, P * (jt + 1))
+            bus = psum.tile([P, KP], F32, tag="acc", name="bus", bufs=4)
+            for a in range(2):
+                nc.tensor.matmul_mx(
+                    out=bus[:], lhsT=got["bus", a][:, js].bitcast(FP8X4), lhsT_scale=(got_sc["bus"], v_sc_hi)[a][:, js],
+                    rhs=bus_w[c][:, a, :].bitcast(FP4X4), rhs_scale=bus_sc[:, a, KP * c : KP * (c + 1)],
+                    start=(a == 0), stop=(a == 1),
+                )
+            diff = ring.tile([P, PACK, P], F32, tag="diff", name="diff", bufs=8)
+            nc.vector.tensor_tensor(
+                out=diff[:].rearrange("j t (u q) -> j t u q", q=4),
+                in0=bus[:].rearrange("j (u t q) -> j t u q", t=PACK, q=4),
+                in1=adj_sb[c, jt][:].rearrange("j t (u q) -> j t u q", q=4),
+                op=ALU.subtract,
+            )
+            diffs[c, jt] = diff
+
+        def sine(c, jt):
+            diff = diffs[c, jt]
+            turned = psum.tile([P, PACK, P], F32, tag="turned", name="turned", bufs=2)
+            for t in range(PACK):
+                nc.tensor.transpose(turned[:, t, :], diff[:, t, :], ident[:])
+            sines[c, jt] = kept([P, P, PACK], F32, "sine%d%d" % (c, jt))
+            nc.scalar.activation(out=sines[c, jt][:], in_=turned[:].rearrange("p t j -> p j t"), func=ACT.Sin)
+
+        bus_sb = {}
+
+        def product(c, jt, name):
+            js = slice(P * jt, P * (jt + 1))
+            cs = slice(KP * c, KP * (c + 1))
+            acc = psum.tile([P, KP], F32, tag="acc", name=name, bufs=4)
+            for a in range(2):
+                if name == "adj":
+                    planes_a = (got_sc["adj"][4 * a :, js], adj_sc[4 * a :, cs])
+                    rhs = adj_w[c][:, a, :].bitcast(FP8X4)
+                else:
+                    planes_a = ((got_sc["bus"], v_sc_hi)[a][:, js], bus_sc[:, a, cs])
+                    rhs = bus_w[c][:, a, :].bitcast(FP4X4)
+                nc.tensor.matmul_mx(
+                    out=acc[:], lhsT=got[name, a][:, js].bitcast(FP8X4), lhsT_scale=planes_a[0],
+                    rhs=rhs, rhs_scale=planes_a[1], start=(a == 0), stop=(a == 1),
+                )
+            sb = ring.tile([P, PACK, P], F32, tag=name + "_sb", name=name + "_sb", bufs=8)
+            nc.scalar.activation(
+                out=sb[:].rearrange("j t (u q) -> j t u q", q=4),
+                in_=acc[:].rearrange("j (u t q) -> j t u q", t=PACK, q=4),
+                func=ACT.Copy, scale=(-1.0 if name == "adj" else 1.0),
+            )
+            (adj_sb if name == "adj" else bus_sb)[c, jt] = sb
+
+        def sine_of_sum(c, jt):
+            turned = psum.tile([P, PACK, P], F32, tag="turned", name="turned", bufs=2)
+            for t in range(PACK):
+                nc.tensor.matmul(turned[:, t, :], lhsT=bus_sb[c, jt][:, t, :], rhs=ident[:], start=True, stop=False, is_transpose=True)
+                nc.tensor.matmul(turned[:, t, :], lhsT=adj_sb[c, jt][:, t, :], rhs=ident[:], start=False, stop=True, is_transpose=True)
+            sines[c, jt] = kept([P, P, PACK], F32, "sine%d%d" % (c, jt))
+            nc.scalar.activation(out=sines[c, jt][:], in_=turned[:].rearrange("p t j -> p j t"), func=ACT.Sin)
+
+        def features(c, jt):
+            js = slice(P * jt, P * (jt + 1))
+            line = psum.tile([P, PACK, P], F32, tag="line", name="line", bufs=2)
+            for t in range(PACK):
+                ms = slice(P * t, P * (t + 1))
+                for a in (1, 0):
+                    codes, sc = wl_q[c, a]
+                    nc.tensor.matmul_mx(
+                        out=line[:, t, :], lhsT=codes[:, ms].bitcast(FP8X4), lhsT_scale=sc[:, ms],
+                        rhs=got["line", a][:, js].bitcast(FP8X4), rhs_scale=got_sc["line"][4 * a :, js],
+                        start=(a == 1), stop=(a == 0),
+                    )
+            hs[c, jt] = kept([P, P, PACK], BF16, "h%d%d" % (c, jt))
+            nc.vector.tensor_tensor(out=hs[c, jt][:], in0=line[:].rearrange("p t j -> p j t"), in1=sines[c, jt][:], op=ALU.mult)
+
+        def quantise_h(c, jt):
+            codes = kept([P, P], U32, "h_w%d%d" % (c, jt))
+            sc = kept([P, P], U8, "h_s%d%d" % (c, jt))
+            nc.vector.quantize_mx(out=codes[:].bitcast(FP8X4), scales=sc[:], in_=hs[c, jt][:].rearrange("p j t -> p (j t)"))
+            h_q[c, jt] = (codes, sc)
+
+        y_w = kept([P, S], U32, "y_w")
+        y_sc = kept([P, S], U8, "y_sc")
+        y_rows = out_0.rearrange("(p t) j -> p t j", t=PACK)
+        y_words = out_1[0].rearrange("p m t -> p (m t)").bitcast(I32)
+        ys = {}
+
+        def project(jt):
+            js = slice(P * jt, P * (jt + 1))
+            flow = psum.tile([P, PACK, P], F32, tag="acc", name="flow", bufs=4)
+            for t in range(PACK):
+                ms = slice(P * t, P * (t + 1))
+                for g in range(2):
+                    codes, sc = ws_q[g]
+                    nc.tensor.matmul_mx(
+                        out=flow[:, t, :], lhsT=codes[:, ms].bitcast(FP8X4), lhsT_scale=sc[:, ms],
+                        rhs=h_q[g, jt][0][:].bitcast(FP8X4), rhs_scale=h_q[g, jt][1][:],
+                        start=(g == 0), stop=(g == 1),
+                    )
+            ys[jt] = kept([P, PACK, P], F32, "y%d" % jt)
+            for t in range(PACK):
+                nc.scalar.activation(
+                    out=ys[jt][:, t, :], in_=flow[:, t, :], func=ACT.Identity,
+                    bias=pin_inv[:, t : t + 1], scale=neg_inv[:, t : t + 1],
+                )
+            nc.sync.dma_start(out=y_rows[:, :, js], in_=ys[jt][:])
+
+        def planes(jt):
+            js = slice(P * jt, P * (jt + 1))
+            y_bf = kept([P, P, PACK], BF16, "y_bf%d" % jt)
+            nc.vector.tensor_copy(
+                out=y_bf[:].rearrange("p (c i) t -> p c t i", i=4),
+                in_=ys[jt][:].rearrange("p t (c i) -> p c t i", i=4),
+            )
+            nc.vector.quantize_mx(out=y_w[:, js].bitcast(FP8X4), scales=y_sc[:, js], in_=y_bf[:].rearrange("p j t -> p (j t)"))
+            nc.sync.dma_start(out=y_words[:, js], in_=y_w[:, js].bitcast(I32))
+
+        def shift_bus_plane(eng):
+            eng.dma_start(out=v_sc_hi[0:100, :].bitcast(I32), in_=got_sc["bus"][4:104, :].bitcast(I32))
+
+        def row_constants(eng):
+            eng.dma_start(out=pin[:], in_=pinj.rearrange("(p t) -> p t", t=PACK))
+            eng.dma_start(out=inv[:], in_=minv.rearrange("(p t) -> p t", t=PACK))
+            nc.gpsimd.tensor_scalar(out=neg_inv[:], in0=inv[:], scalar1=-1.0, scalar2=0.0, op0=ALU.mult, op1=ALU.add)
+            nc.gpsimd.tensor_tensor(out=pin_inv[:], in0=pin[:], in1=inv[:], op=ALU.mult)
+
+        def scales_out():
+            for q in range(QUADS):
+                (nc.scalar, nc.sync)[q % 2].dma_start(
+                    out=out_2[0, 4 * q : 4 * q + 4, :].bitcast(I32),
+                    in_=y_sc[32 * q : 32 * q + 4, :].bitcast(I32),
+                )
+
+        on_scalar, on_vector = nc.scalar.copy, nc.vector.tensor_copy
+
+        nc.gpsimd.memset(tab_sc[:].bitcast(I32), 0)
+        nc.vector.memset(bus_sc[:].bitcast(I32), 0)
+        nc.vector.memset(adj_sc[:].bitcast(I32), 0)
+        nc.vector.memset(v_sc_hi[:].bitcast(I32), 0)
+        nc.vector.memset(warm[:], 0.0)
+        tab_scales_in(nc.scalar)
+        load_list("bus", offs)
+        load_list("adj", offs2)
+        load_tab(0)
+        load_tab(1)
+        adj_scales_in(nc.scalar)
+        nc.scalar.activation(out=warm2[:], in_=warm[:], func=ACT.Sin)
+        bus_scales_in(nc.gpsimd)
+        make_identity(nc, ident[:])
+        load_adj(0)
+        load_bus(0)
+        load_list("line", offs3)
+        load_line(0, 0)
+        load_adj(1)
+        load_bus(1)
+        load_line(0, 1)
+        load_line(1, 0)
+        load_line(1, 1)
+        row_constants(nc.sync)
+        load_state(0)
+        load_state(1)
+        gather_scales("bus")
+        shift_bus_plane(nc.gpsimd)
+        gather_scales("adj")
+        gather_words("adj", 0)
+        gather_words("bus", 0)
+        gather_words("adj", 1)
+        gather_words("bus", 1)
+        gather_scales("line")
+        gather_words("line", 0)
+        gather_words("line", 1)
+        for jt in range(JT):
+            adjacent(0, jt)
+            angle(0, jt)
+        for jt in range(JT):
+            adjacent(1, jt)
+            angle(1, jt)
+            sine(0, jt)
+        round_line(0, 0, on_scalar, on_scalar)
+        round_line(0, 1, on_vector)
+        quantise_line(0, 0)
+        quantise_line(0, 1)
+        round_line(1, 0, on_scalar, on_scalar)
+        round_line(1, 1, on_scalar, on_vector)
+        quantise_line(1, 0)
+        quantise_line(1, 1)
+        for jt in range(JT):
+            features(0, jt)
+            sine(1, jt)
+        round_state(0, on_scalar, on_scalar)
+        round_state(1, on_scalar, on_vector)
+        quantise_state(0)
+        for jt in range(JT):
+            features(1, jt)
+        for c in range(2):
+            for jt in range(JT):
+                quantise_h(c, jt)
+        quantise_state(1)
+        for jt in range(JT):
+            project(jt)
+        for jt in range(JT):
+            planes(jt)
+        scales_out()

@@ -19,9 +19,12 @@ ALU = mybir.AluOpType
 
 P = 128
 PACK = 4
-KP = P * PACK
+PASS = P * PACK
+PASSES = 2
 QUADS = 4
-JT = S // P
+TILES = S // P
+RUN = 4
+SHIFTED_ROWS = 100
 
 
 def tile_list_grid_swing_flow_kernel(
@@ -31,335 +34,286 @@ def tile_list_grid_swing_flow_kernel(
     nc = tc.nc
     with ExitStack() as ctx:
         keep = ctx.enter_context(tc.tile_pool(name="keep", bufs=1))
-        ring = ctx.enter_context(tc.tile_pool(name="ring", bufs=3))
         psum = ctx.enter_context(tc.psum_pool(name="psum", bufs=2))
 
         def kept(shape, dtype, name):
             return keep.tile(shape, dtype, name=name, align_bytes=64)
 
         tab_sc = kept([P, T], U8, "tab_sc")
-        adj_sc = kept([P, H], U8, "adj_sc")
-        bus_sc = kept([P, 2, H], U8, "bus_sc")
-        v_sc_hi = kept([P, S], U8, "v_sc_hi")
-        warm = kept([P, 1], F32, "warm")
-        warm2 = kept([P, 1], F32, "warm2")
+        adj_sc = kept([P, PASSES, H], U8, "adj_sc")
+        bus_sc = kept([P, PASSES, H], U8, "bus_sc")
+        bus_picked_sc1 = kept([P, S], U8, "bus_picked_sc1")
+        warm_in = kept([P, 1], F32, "warm_in")
+        warm_out = kept([P, 1], F32, "warm_out")
         ident = kept([P, P], F32, "ident")
         pin = kept([P, PACK], F32, "pin")
         inv = kept([P, PACK], F32, "inv")
         neg_inv = kept([P, PACK], F32, "neg_inv")
         pin_inv = kept([P, PACK], F32, "pin_inv")
-        lists = {}
-        wl_raw, adj_w, bus_w, tab_w, ws_raw = {}, {}, {}, {}, {}
-        wl_bf, wl_q, ws_bf, ws_q, got, got_sc, sines, hs, h_q = {}, {}, {}, {}, {}, {}, {}, {}, {}
+        h_first = kept([P, S, PACK], BF16, "h_first")
+        y_words = kept([P, S], U32, "y_words")
+        y_sc = kept([P, S], U8, "y_sc")
+        lists, tab_w, adj_w, bus_w, line_raw, state_raw = {}, {}, {}, {}, {}, {}
+        picked, picked_sc, line_bf, state_bf, line_q, state_q = {}, {}, {}, {}, {}, {}
+        adj_sb, diffs, sines, h_bf, h_q, ys = {}, {}, {}, {}, {}, {}
 
         def load_list(name, src):
             lists[name] = keep.tile([P, S // 16], U16, name="list_" + name)
             nc.sync.dma_start(lists[name][:], src)
 
-        def tab_scales_in(eng):
+        def load_table_scales():
             for q in range(QUADS):
-                eng.dma_start(
+                nc.sync.dma_start(
                     out=tab_sc[32 * q : 32 * q + 8, :].bitcast(I32),
                     in_=tab_scales[:, 4 * q : 4 * q + 4, :].bitcast(I32),
                 )
 
-        def adj_scales_in(eng):
+        def load_weight_scales(planes, scales):
             for q in range(QUADS):
-                eng.dma_start(
-                    out=adj_sc[32 * q : 32 * q + 8, :].bitcast(I32),
-                    in_=wadj_scales[:, 4 * q : 4 * q + 4, :].bitcast(I32),
+                nc.scalar.dma_start(
+                    out=planes[32 * q : 32 * q + 4, :, :].bitcast(I32),
+                    in_=scales[:, 4 * q : 4 * q + 4, :].rearrange("a r c -> r a c").bitcast(I32),
                 )
 
-        def bus_scales_in(eng):
-            for q in range(QUADS):
-                eng.dma_start(
-                    out=bus_sc[32 * q : 32 * q + 4, :, :].bitcast(I32),
-                    in_=wbus_scales[:, 4 * q : 4 * q + 4, :].rearrange("a r c -> r a c").bitcast(I32),
-                )
-
-        def load_tab(a):
+        def load_table(a):
             tab_w[a] = kept([P, T], U32, "tab_w%d" % a)
             nc.sync.dma_start(out=tab_w[a][:].bitcast(I32), in_=tab_words[a].rearrange("p t i -> p (t i)").bitcast(I32))
 
         def load_adj(c):
-            adj_w[c] = kept([P, 2, KP], U32, "adj_w%d" % c)
-            nc.sync.dma_start(
-                out=adj_w[c][:].bitcast(I32),
-                in_=wadj_words.rearrange("a p c i -> p a (c i)")[:, :, 4 * KP * c : 4 * KP * (c + 1)].bitcast(I32),
-            )
+            adj_w[c] = kept([P, PASSES, PASS], U32, "adj_w%d" % c)
+            words = wadj_words.rearrange("a p c i -> p a (c i)")
+            nc.sync.dma_start(out=adj_w[c][:].bitcast(I32), in_=words[:, :, 4 * PASS * c : 4 * PASS * (c + 1)].bitcast(I32))
 
         def load_bus(c):
-            bus_w[c] = kept([P, 2, 2 * KP], U8, "bus_w%d" % c)
-            nc.sync.dma_start(
-                out=bus_w[c][:].bitcast(I32),
-                in_=wbus_words.rearrange("a p c -> p a c")[:, :, 2 * KP * c : 2 * KP * (c + 1)].bitcast(I32),
-            )
+            bus_w[c] = kept([P, PASSES, 2 * PASS], U8, "bus_w%d" % c)
+            words = wbus_words.rearrange("a p c -> p a c")
+            nc.sync.dma_start(out=bus_w[c][:].bitcast(I32), in_=words[:, :, 2 * PASS * c : 2 * PASS * (c + 1)].bitcast(I32))
 
         def load_line(c, a):
-            wl_raw[c, a] = kept([P, PACK, KP], F32, "wl_raw%d%d" % (c, a))
-            rows = wline[KP * a : KP * (a + 1), KP * c : KP * (c + 1)]
-            nc.sync.dma_start(out=wl_raw[c, a][:], in_=rows.rearrange("(p i) c -> p i c", i=PACK))
+            line_raw[c, a] = kept([P, PACK, PASS], F32, "line_raw%d%d" % (c, a))
+            rows = wline[PASS * a : PASS * (a + 1), PASS * c : PASS * (c + 1)]
+            nc.sync.dma_start(out=line_raw[c, a][:], in_=rows.rearrange("(p i) r -> p i r", i=PACK))
 
-        def load_state(g):
-            ws_raw[g] = kept([P, PACK, N], F32, "ws_raw%d" % g)
-            rows = wstate[KP * g : KP * (g + 1), :].rearrange("(u t q) n -> t u q n", t=PACK, q=4)
+        def load_state(c):
+            state_raw[c] = kept([P, PACK, N], F32, "state_raw%d" % c)
+            rows = wstate[PASS * c : PASS * (c + 1), :].rearrange("(u t e) n -> t u e n", t=PACK, e=RUN)
             for t in range(PACK):
-                nc.sync.dma_start(out=ws_raw[g][:, t, :], in_=rows[t])
+                nc.sync.dma_start(out=state_raw[c][:, t, :], in_=rows[t])
 
         def gather_scales(name):
-            got_sc[name] = kept([P, S], U8, "picked_sc_" + name)
-            nc.vector.tensor_copy(got_sc[name][:], tab_sc[:].indirect(lists[name][:]))
+            picked_sc[name] = kept([P, S], U8, "picked_sc_" + name)
+            nc.vector.tensor_copy(picked_sc[name][:], tab_sc[:].indirect(lists[name][:]))
 
         def gather_words(name, a):
-            got[name, a] = kept([P, S], U32, "%s_v%d" % (name, a))
-            nc.vector.tensor_copy(got[name, a][:], tab_w[a][:].indirect(lists[name][:]))
+            picked[name, a] = kept([P, S], U32, "picked_%s%d" % (name, a))
+            nc.vector.tensor_copy(picked[name, a][:], tab_w[a][:].indirect(lists[name][:]))
+
+        def shift_bus_plane():
+            nc.sync.dma_start(
+                out=bus_picked_sc1[0:SHIFTED_ROWS, :].bitcast(I32),
+                in_=picked_sc["bus"][4 : 4 + SHIFTED_ROWS, :].bitcast(I32),
+            )
 
         def round_line(c, a, *copies):
-            wl_bf[c, a] = kept([P, PACK, P, PACK], BF16, "wl_bf%d%d" % (c, a))
-            w = 32 // len(copies)
-            for n, copy in enumerate(copies):
+            line_bf[c, a] = kept([P, PACK, P, PACK], BF16, "line_bf%d%d" % (c, a))
+            share = P // RUN // len(copies)
+            for part, copy in enumerate(copies):
+                us = slice(share * part, share * (part + 1))
                 copy(
-                    out=wl_bf[c, a][:].rearrange("p t (u q) i -> p u t i q", q=4)[:, w * n : w * (n + 1)],
-                    in_=wl_raw[c, a][:].rearrange("p i (u t q) -> p u t i q", t=PACK, q=4)[:, w * n : w * (n + 1)],
+                    out=line_bf[c, a][:].rearrange("p t (u e) i -> p u t i e", e=RUN)[:, us],
+                    in_=line_raw[c, a][:].rearrange("p i (u t e) -> p u t i e", t=PACK, e=RUN)[:, us],
                 )
 
-        def round_state(g, *copies):
-            ws_bf[g] = kept([P, PACK, P, PACK], BF16, "ws_bf%d" % g)
-            w = P // len(copies)
-            for n, copy in enumerate(copies):
-                copy(
-                    out=ws_bf[g][:].rearrange("p t m i -> p m i t")[:, w * n : w * (n + 1)],
-                    in_=ws_raw[g][:].rearrange("p i (m t) -> p m i t", t=PACK)[:, w * n : w * (n + 1)],
-                )
+        def round_state(c):
+            state_bf[c] = kept([P, PACK, P, PACK], BF16, "state_bf%d" % c)
+            nc.scalar.copy(
+                out=state_bf[c][:].rearrange("p t m s -> p m s t"),
+                in_=state_raw[c][:].rearrange("p s (m t) -> p m s t", t=PACK),
+            )
 
-        def quantise(bf, name):
-            codes = kept([P, KP], U32, name + "_w")
-            sc = kept([P, KP], U8, name + "_s")
-            nc.vector.quantize_mx(out=codes[:].bitcast(FP8X4), scales=sc[:], in_=bf[:].rearrange("p t m i -> p (t m i)"))
-            return codes, sc
+        def quantise(values, name):
+            columns = values.shape[1] // PACK
+            codes = kept([P, columns], U32, name + "_words")
+            plane = kept([P, columns], U8, name + "_sc")
+            nc.vector.quantize_mx(out=codes[:].bitcast(FP8X4), scales=plane[:], in_=values)
+            return codes, plane
 
         def quantise_line(c, a):
-            wl_q[c, a] = quantise(wl_bf[c, a], "wl_q%d%d" % (c, a))
+            line_q[c, a] = quantise(line_bf[c, a][:].rearrange("p t m i -> p (t m i)"), "line%d%d" % (c, a))
 
-        def quantise_state(g):
-            ws_q[g] = quantise(ws_bf[g], "ws_q%d" % g)
+        def quantise_state(c):
+            state_q[c] = quantise(state_bf[c][:].rearrange("p t m s -> p (t m s)"), "state%d" % c)
 
-        adj_sb, diffs = {}, {}
+        def by_slot(ap):
+            return ap.rearrange("j (u t e) -> j t u e", t=PACK, e=RUN)
 
         def adjacent(c, jt):
             js = slice(P * jt, P * (jt + 1))
-            adj = psum.tile([P, KP], F32, tag="acc", name="adj", bufs=4)
-            for a in range(2):
+            adj = psum.tile([P, PASS], F32, tag="adj_or_flow", name="adj")
+            for a in range(PASSES):
                 nc.tensor.matmul_mx(
-                    out=adj[:], lhsT=got["adj", a][:, js].bitcast(FP8X4), lhsT_scale=got_sc["adj"][4 * a :, js],
-                    rhs=adj_w[c][:, a, :].bitcast(FP8X4), rhs_scale=adj_sc[4 * a :, KP * c : KP * (c + 1)],
-                    start=(a == 0), stop=(a == 1),
+                    out=adj[:], lhsT=picked["adj", a][:, js].bitcast(FP8X4), lhsT_scale=picked_sc["adj"][4 * a :, js],
+                    rhs=adj_w[c][:, a, :].bitcast(FP8X4), rhs_scale=adj_sc[:, a, PASS * c : PASS * (c + 1)],
+                    start=(a == 0), stop=(a == PASSES - 1),
                 )
-            adj_sb[c, jt] = ring.tile([P, PACK, P], F32, tag="adj_sb", name="adj_sb", bufs=8)
-            nc.scalar.copy(
-                out=adj_sb[c, jt][:].rearrange("j t (u q) -> j t u q", q=4),
-                in_=adj[:].rearrange("j (u t q) -> j t u q", t=PACK, q=4),
-            )
+            adj_sb[c, jt] = kept([P, PACK, P], F32, "adj_sb%d%d" % (c, jt))
+            nc.scalar.copy(out=adj_sb[c, jt][:].rearrange("j t (u e) -> j t u e", e=RUN), in_=by_slot(adj[:]))
 
-        def angle(c, jt):
+        def difference(c, jt):
             js = slice(P * jt, P * (jt + 1))
-            bus = psum.tile([P, KP], F32, tag="acc", name="bus", bufs=4)
-            for a in range(2):
+            bus = psum.tile([P, PASS], F32, tag="bus_or_flow", name="bus")
+            for a in range(PASSES):
                 nc.tensor.matmul_mx(
-                    out=bus[:], lhsT=got["bus", a][:, js].bitcast(FP8X4), lhsT_scale=(got_sc["bus"], v_sc_hi)[a][:, js],
-                    rhs=bus_w[c][:, a, :].bitcast(FP4X4), rhs_scale=bus_sc[:, a, KP * c : KP * (c + 1)],
-                    start=(a == 0), stop=(a == 1),
+                    out=bus[:], lhsT=picked["bus", a][:, js].bitcast(FP8X4),
+                    lhsT_scale=(picked_sc["bus"], bus_picked_sc1)[a][:, js],
+                    rhs=bus_w[c][:, a, :].bitcast(FP4X4), rhs_scale=bus_sc[:, a, PASS * c : PASS * (c + 1)],
+                    start=(a == 0), stop=(a == PASSES - 1),
                 )
-            diff = ring.tile([P, PACK, P], F32, tag="diff", name="diff", bufs=8)
+            diffs[c, jt] = kept([P, PACK, P], F32, "diff%d%d" % (c, jt))
             nc.vector.tensor_tensor(
-                out=diff[:].rearrange("j t (u q) -> j t u q", q=4),
-                in0=bus[:].rearrange("j (u t q) -> j t u q", t=PACK, q=4),
-                in1=adj_sb[c, jt][:].rearrange("j t (u q) -> j t u q", q=4),
-                op=ALU.subtract,
+                out=diffs[c, jt][:].rearrange("j t (u e) -> j t u e", e=RUN), in0=by_slot(bus[:]),
+                in1=adj_sb[c, jt][:].rearrange("j t (u e) -> j t u e", e=RUN), op=ALU.subtract,
             )
-            diffs[c, jt] = diff
 
         def sine(c, jt):
-            diff = diffs[c, jt]
-            turned = psum.tile([P, PACK, P], F32, tag="turned", name="turned", bufs=2)
+            turned = psum.tile([P, PACK, P], F32, tag="turned", name="turned")
             for t in range(PACK):
-                nc.tensor.transpose(turned[:, t, :], diff[:, t, :], ident[:])
-            sines[c, jt] = kept([P, P, PACK], F32, "sine%d%d" % (c, jt))
-            nc.scalar.activation(out=sines[c, jt][:], in_=turned[:].rearrange("p t j -> p j t"), func=ACT.Sin)
-
-        bus_sb = {}
-
-        def product(c, jt, name):
-            js = slice(P * jt, P * (jt + 1))
-            cs = slice(KP * c, KP * (c + 1))
-            acc = psum.tile([P, KP], F32, tag="acc", name=name, bufs=4)
-            for a in range(2):
-                if name == "adj":
-                    planes_a = (got_sc["adj"][4 * a :, js], adj_sc[4 * a :, cs])
-                    rhs = adj_w[c][:, a, :].bitcast(FP8X4)
-                else:
-                    planes_a = ((got_sc["bus"], v_sc_hi)[a][:, js], bus_sc[:, a, cs])
-                    rhs = bus_w[c][:, a, :].bitcast(FP4X4)
-                nc.tensor.matmul_mx(
-                    out=acc[:], lhsT=got[name, a][:, js].bitcast(FP8X4), lhsT_scale=planes_a[0],
-                    rhs=rhs, rhs_scale=planes_a[1], start=(a == 0), stop=(a == 1),
-                )
-            sb = ring.tile([P, PACK, P], F32, tag=name + "_sb", name=name + "_sb", bufs=8)
-            nc.scalar.activation(
-                out=sb[:].rearrange("j t (u q) -> j t u q", q=4),
-                in_=acc[:].rearrange("j (u t q) -> j t u q", t=PACK, q=4),
-                func=ACT.Copy, scale=(-1.0 if name == "adj" else 1.0),
-            )
-            (adj_sb if name == "adj" else bus_sb)[c, jt] = sb
-
-        def sine_of_sum(c, jt):
-            turned = psum.tile([P, PACK, P], F32, tag="turned", name="turned", bufs=2)
-            for t in range(PACK):
-                nc.tensor.matmul(turned[:, t, :], lhsT=bus_sb[c, jt][:, t, :], rhs=ident[:], start=True, stop=False, is_transpose=True)
-                nc.tensor.matmul(turned[:, t, :], lhsT=adj_sb[c, jt][:, t, :], rhs=ident[:], start=False, stop=True, is_transpose=True)
+                nc.tensor.transpose(turned[:, t, :], diffs[c, jt][:, t, :], ident[:])
             sines[c, jt] = kept([P, P, PACK], F32, "sine%d%d" % (c, jt))
             nc.scalar.activation(out=sines[c, jt][:], in_=turned[:].rearrange("p t j -> p j t"), func=ACT.Sin)
 
         def features(c, jt):
             js = slice(P * jt, P * (jt + 1))
-            line = psum.tile([P, PACK, P], F32, tag="line", name="line", bufs=2)
+            line = psum.tile([P, PACK, P], F32, tag="line", name="line")
             for t in range(PACK):
                 ms = slice(P * t, P * (t + 1))
                 for a in (1, 0):
-                    codes, sc = wl_q[c, a]
+                    codes, plane = line_q[c, a]
                     nc.tensor.matmul_mx(
-                        out=line[:, t, :], lhsT=codes[:, ms].bitcast(FP8X4), lhsT_scale=sc[:, ms],
-                        rhs=got["line", a][:, js].bitcast(FP8X4), rhs_scale=got_sc["line"][4 * a :, js],
+                        out=line[:, t, :], lhsT=codes[:, ms].bitcast(FP8X4), lhsT_scale=plane[:, ms],
+                        rhs=picked["line", a][:, js].bitcast(FP8X4), rhs_scale=picked_sc["line"][4 * a :, js],
                         start=(a == 1), stop=(a == 0),
                     )
-            hs[c, jt] = kept([P, P, PACK], BF16, "h%d%d" % (c, jt))
-            nc.vector.tensor_tensor(out=hs[c, jt][:], in0=line[:].rearrange("p t j -> p j t"), in1=sines[c, jt][:], op=ALU.mult)
+            h_bf[c, jt] = h_first[:, js, :] if c == 0 else kept([P, P, PACK], BF16, "h_last%d" % jt)[:]
+            nc.vector.tensor_tensor(out=h_bf[c, jt], in0=line[:].rearrange("p t j -> p j t"), in1=sines[c, jt][:], op=ALU.mult)
 
-        def quantise_h(c, jt):
-            codes = kept([P, P], U32, "h_w%d%d" % (c, jt))
-            sc = kept([P, P], U8, "h_s%d%d" % (c, jt))
-            nc.vector.quantize_mx(out=codes[:].bitcast(FP8X4), scales=sc[:], in_=hs[c, jt][:].rearrange("p j t -> p (j t)"))
-            h_q[c, jt] = (codes, sc)
+        def quantise_h_first():
+            codes, plane = quantise(h_first[:].rearrange("p j t -> p (j t)"), "h_first")
+            for jt in range(TILES):
+                h_q[0, jt] = (codes[:, P * jt : P * (jt + 1)], plane[:, P * jt : P * (jt + 1)])
 
-        y_w = kept([P, S], U32, "y_w")
-        y_sc = kept([P, S], U8, "y_sc")
-        y_rows = out_0.rearrange("(p t) j -> p t j", t=PACK)
-        y_words = out_1[0].rearrange("p m t -> p (m t)").bitcast(I32)
-        ys = {}
+        def quantise_h_last(jt):
+            codes, plane = quantise(h_bf[1, jt].rearrange("p j t -> p (j t)"), "h_last%d" % jt)
+            h_q[1, jt] = (codes[:], plane[:])
 
         def project(jt):
-            js = slice(P * jt, P * (jt + 1))
-            flow = psum.tile([P, PACK, P], F32, tag="acc", name="flow", bufs=4)
+            banks = [psum.tile([P, 2, P], F32, tag=tag, name="flow") for tag in ("adj_or_flow", "bus_or_flow")]
             for t in range(PACK):
                 ms = slice(P * t, P * (t + 1))
-                for g in range(2):
-                    codes, sc = ws_q[g]
+                for c in (1, 0):
+                    codes, plane = state_q[c]
                     nc.tensor.matmul_mx(
-                        out=flow[:, t, :], lhsT=codes[:, ms].bitcast(FP8X4), lhsT_scale=sc[:, ms],
-                        rhs=h_q[g, jt][0][:].bitcast(FP8X4), rhs_scale=h_q[g, jt][1][:],
-                        start=(g == 0), stop=(g == 1),
+                        out=banks[t // 2][:, t % 2, :], lhsT=codes[:, ms].bitcast(FP8X4), lhsT_scale=plane[:, ms],
+                        rhs=h_q[c, jt][0].bitcast(FP8X4), rhs_scale=h_q[c, jt][1],
+                        start=(c == 1), stop=(c == 0),
                     )
             ys[jt] = kept([P, PACK, P], F32, "y%d" % jt)
             for t in range(PACK):
                 nc.scalar.activation(
-                    out=ys[jt][:, t, :], in_=flow[:, t, :], func=ACT.Identity,
+                    out=ys[jt][:, t, :], in_=banks[t // 2][:, t % 2, :], func=ACT.Identity,
                     bias=pin_inv[:, t : t + 1], scale=neg_inv[:, t : t + 1],
                 )
-            nc.sync.dma_start(out=y_rows[:, :, js], in_=ys[jt][:])
+            rows = out_0.rearrange("(p t) j -> p t j", t=PACK)
+            nc.sync.dma_start(out=rows[:, :, P * jt : P * (jt + 1)], in_=ys[jt][:])
 
         def planes(jt):
             js = slice(P * jt, P * (jt + 1))
             y_bf = kept([P, P, PACK], BF16, "y_bf%d" % jt)
             nc.vector.tensor_copy(
-                out=y_bf[:].rearrange("p (c i) t -> p c t i", i=4),
-                in_=ys[jt][:].rearrange("p t (c i) -> p c t i", i=4),
+                out=y_bf[:].rearrange("p (g e) t -> p g t e", e=RUN),
+                in_=ys[jt][:].rearrange("p t (g e) -> p g t e", e=RUN),
             )
-            nc.vector.quantize_mx(out=y_w[:, js].bitcast(FP8X4), scales=y_sc[:, js], in_=y_bf[:].rearrange("p j t -> p (j t)"))
-            nc.sync.dma_start(out=y_words[:, js], in_=y_w[:, js].bitcast(I32))
-
-        def shift_bus_plane(eng):
-            eng.dma_start(out=v_sc_hi[0:100, :].bitcast(I32), in_=got_sc["bus"][4:104, :].bitcast(I32))
-
-        def row_constants(eng):
-            eng.dma_start(out=pin[:], in_=pinj.rearrange("(p t) -> p t", t=PACK))
-            eng.dma_start(out=inv[:], in_=minv.rearrange("(p t) -> p t", t=PACK))
-            nc.gpsimd.tensor_scalar(out=neg_inv[:], in0=inv[:], scalar1=-1.0, scalar2=0.0, op0=ALU.mult, op1=ALU.add)
-            nc.gpsimd.tensor_tensor(out=pin_inv[:], in0=pin[:], in1=inv[:], op=ALU.mult)
-
-        def scales_out():
-            for q in range(QUADS):
-                (nc.scalar, nc.sync)[q % 2].dma_start(
-                    out=out_2[0, 4 * q : 4 * q + 4, :].bitcast(I32),
-                    in_=y_sc[32 * q : 32 * q + 4, :].bitcast(I32),
-                )
+            nc.vector.quantize_mx(out=y_words[:, js].bitcast(FP8X4), scales=y_sc[:, js], in_=y_bf[:].rearrange("p j t -> p (j t)"))
+            words_out = out_1[0].rearrange("p j t -> p (j t)").bitcast(I32)
+            queue = nc.scalar if jt == TILES - 1 else nc.sync
+            queue.dma_start(out=words_out[:, js], in_=y_words[:, js].bitcast(I32))
 
         on_scalar, on_vector = nc.scalar.copy, nc.vector.tensor_copy
 
         nc.gpsimd.memset(tab_sc[:].bitcast(I32), 0)
-        nc.vector.memset(bus_sc[:].bitcast(I32), 0)
+        nc.vector.memset(warm_in[:], 0.0)
+        nc.vector.memset(bus_picked_sc1[:].bitcast(I32), 0)
         nc.vector.memset(adj_sc[:].bitcast(I32), 0)
-        nc.vector.memset(v_sc_hi[:].bitcast(I32), 0)
-        nc.vector.memset(warm[:], 0.0)
-        tab_scales_in(nc.scalar)
-        load_list("bus", offs)
-        load_list("adj", offs2)
-        load_tab(0)
-        load_tab(1)
-        adj_scales_in(nc.scalar)
-        nc.scalar.activation(out=warm2[:], in_=warm[:], func=ACT.Sin)
-        bus_scales_in(nc.gpsimd)
+        nc.vector.memset(bus_sc[:].bitcast(I32), 0)
+        nc.gpsimd.dma_start(out=pin[:], in_=pinj.rearrange("(p t) -> p t", t=PACK))
+        nc.gpsimd.dma_start(out=inv[:], in_=minv.rearrange("(p t) -> p t", t=PACK))
+        nc.gpsimd.tensor_scalar(out=neg_inv[:], in0=inv[:], scalar1=-1.0, scalar2=0.0, op0=ALU.mult, op1=ALU.add)
+        nc.gpsimd.tensor_tensor(out=pin_inv[:], in0=pin[:], in1=inv[:], op=ALU.mult)
         make_identity(nc, ident[:])
+        nc.scalar.activation(out=warm_out[:], in_=warm_in[:], func=ACT.Sin)
+
+        load_list("bus", offs)
+        load_table_scales()
+        load_list("adj", offs2)
+        load_table(0)
+        load_table(1)
+        gather_scales("bus")
         load_adj(0)
-        load_bus(0)
+        shift_bus_plane()
         load_list("line", offs3)
-        load_line(0, 0)
         load_adj(1)
+        load_bus(0)
+        load_line(0, 0)
         load_bus(1)
         load_line(0, 1)
         load_line(1, 0)
-        load_line(1, 1)
-        row_constants(nc.sync)
         load_state(0)
+        load_line(1, 1)
         load_state(1)
-        gather_scales("bus")
-        shift_bus_plane(nc.gpsimd)
+        load_weight_scales(adj_sc, wadj_scales)
+        load_weight_scales(bus_sc, wbus_scales)
+
         gather_scales("adj")
-        gather_words("adj", 0)
-        gather_words("bus", 0)
-        gather_words("adj", 1)
-        gather_words("bus", 1)
+        for a in range(PASSES):
+            gather_words("adj", a)
+            gather_words("bus", a)
         gather_scales("line")
-        gather_words("line", 0)
-        gather_words("line", 1)
-        for jt in range(JT):
+        for a in range(PASSES):
+            gather_words("line", a)
+
+        for jt in range(TILES):
             adjacent(0, jt)
-            angle(0, jt)
-        for jt in range(JT):
+        for jt in range(TILES):
+            difference(0, jt)
+        for jt in range(TILES):
             adjacent(1, jt)
-            angle(1, jt)
+        for jt in range(TILES):
             sine(0, jt)
-        round_line(0, 0, on_scalar, on_scalar)
+        round_line(0, 0, on_scalar)
         round_line(0, 1, on_vector)
         quantise_line(0, 0)
         quantise_line(0, 1)
-        round_line(1, 0, on_scalar, on_scalar)
-        round_line(1, 1, on_scalar, on_vector)
-        quantise_line(1, 0)
-        quantise_line(1, 1)
-        for jt in range(JT):
-            features(0, jt)
+        for jt in range(TILES):
+            difference(1, jt)
+        for jt in range(TILES):
             sine(1, jt)
-        round_state(0, on_scalar, on_scalar)
-        round_state(1, on_scalar, on_vector)
+        round_state(0)
+        round_state(1)
+        round_line(1, 0, on_scalar, on_vector)
+        quantise_line(1, 0)
+        round_line(1, 1, on_vector)
+        quantise_line(1, 1)
         quantise_state(0)
-        for jt in range(JT):
-            features(1, jt)
-        for c in range(2):
-            for jt in range(JT):
-                quantise_h(c, jt)
         quantise_state(1)
-        for jt in range(JT):
+        for jt in range(TILES):
+            features(0, jt)
+        quantise_h_first()
+        for jt in range(TILES):
+            features(1, jt)
+            quantise_h_last(jt)
             project(jt)
-        for jt in range(JT):
+        for jt in range(TILES):
             planes(jt)
-        scales_out()
+        for q in range(QUADS):
+            queue = nc.scalar if q == QUADS - 1 else nc.sync
+            queue.dma_start(out=out_2[0, 4 * q : 4 * q + 4, :].bitcast(I32), in_=y_sc[32 * q : 32 * q + 4, :].bitcast(I32))

@@ -34,7 +34,12 @@ def tile_list_grid_swing_flow_kernel(
     nc = tc.nc
     with ExitStack() as ctx:
         keep = ctx.enter_context(tc.tile_pool(name="keep", bufs=1))
-        psum = ctx.enter_context(tc.psum_pool(name="psum", bufs=2))
+        psum = ctx.enter_context(tc.psum_pool(name="psum", bufs=1))
+
+        banks = [psum.tile([P, PASS], F32, name="bank%d" % b) for b in range(8)]
+
+        def by_group(bank):
+            return bank[:].rearrange("p (t j) -> p t j", t=PACK)
 
         def kept(shape, dtype, name):
             return keep.tile(shape, dtype, name=name, align_bytes=64)
@@ -51,11 +56,12 @@ def tile_list_grid_swing_flow_kernel(
         neg_inv = kept([P, PACK], F32, "neg_inv")
         pin_inv = kept([P, PACK], F32, "pin_inv")
         h_first = kept([P, S, PACK], BF16, "h_first")
+        y_all = kept([P, PACK, S], F32, "y_all")
         y_words = kept([P, S], U32, "y_words")
         y_sc = kept([P, S], U8, "y_sc")
         lists, tab_w, adj_w, bus_w, line_raw, state_raw = {}, {}, {}, {}, {}, {}
         picked, picked_sc, line_bf, state_bf, line_q, state_q = {}, {}, {}, {}, {}, {}
-        adj_sb, diffs, sines, h_bf, h_q, ys = {}, {}, {}, {}, {}, {}
+        adj_sb, diffs, sines, h_bf, h_q, ys, flows = {}, {}, {}, {}, {}, {}, {}
 
         def load_list(name, src):
             lists[name] = keep.tile([P, S // 16], U16, name="list_" + name)
@@ -68,9 +74,9 @@ def tile_list_grid_swing_flow_kernel(
                     in_=tab_scales[:, 4 * q : 4 * q + 4, :].bitcast(I32),
                 )
 
-        def load_weight_scales(planes, scales):
+        def load_weight_scales(planes, scales, queue):
             for q in range(QUADS):
-                nc.scalar.dma_start(
+                queue.dma_start(
                     out=planes[32 * q : 32 * q + 4, :, :].bitcast(I32),
                     in_=scales[:, 4 * q : 4 * q + 4, :].rearrange("a r c -> r a c").bitcast(I32),
                 )
@@ -94,6 +100,12 @@ def tile_list_grid_swing_flow_kernel(
             rows = wline[PASS * a : PASS * (a + 1), PASS * c : PASS * (c + 1)]
             nc.sync.dma_start(out=line_raw[c, a][:], in_=rows.rearrange("(p i) r -> p i r", i=PACK))
 
+        def load_line_pass(a):
+            both = kept([P, PACK, H], F32, "line_raw%d" % a)
+            nc.sync.dma_start(out=both[:], in_=wline[PASS * a : PASS * (a + 1), :].rearrange("(p i) r -> p i r", i=PACK))
+            for c in range(PASSES):
+                line_raw[c, a] = both[:, :, PASS * c : PASS * (c + 1)]
+
         def load_state(c):
             state_raw[c] = kept([P, PACK, N], F32, "state_raw%d" % c)
             rows = wstate[PASS * c : PASS * (c + 1), :].rearrange("(u t e) n -> t u e n", t=PACK, e=RUN)
@@ -104,32 +116,51 @@ def tile_list_grid_swing_flow_kernel(
             picked_sc[name] = kept([P, S], U8, "picked_sc_" + name)
             nc.vector.tensor_copy(picked_sc[name][:], tab_sc[:].indirect(lists[name][:]))
 
-        def gather_words(name, a):
-            picked[name, a] = kept([P, S], U32, "picked_%s%d" % (name, a))
-            nc.vector.tensor_copy(picked[name, a][:], tab_w[a][:].indirect(lists[name][:]))
+        def gather_words(name, a, half=None):
+            if (name, a) not in picked:
+                picked[name, a] = kept([P, S], U32, "picked_%s%d" % (name, a))
+            if half is None:
+                nc.vector.tensor_copy(picked[name, a][:], tab_w[a][:].indirect(lists[name][:]))
+            else:
+                nc.vector.tensor_copy(
+                    picked[name, a][:, S // 2 * half : S // 2 * (half + 1)],
+                    tab_w[a][:].indirect(lists[name][:, S // 32 * half : S // 32 * (half + 1)]),
+                )
+
+        def load_constants():
+            nc.sync.dma_start(out=pin[:], in_=pinj.rearrange("(p t) -> p t", t=PACK))
+            nc.sync.dma_start(out=inv[:], in_=minv.rearrange("(p t) -> p t", t=PACK))
+            nc.scalar.activation(out=neg_inv[:], in_=inv[:], func=ACT.Copy, scale=-1.0)
+            for t in range(PACK):
+                nc.scalar.activation(out=pin_inv[:, t : t + 1], in_=pin[:, t : t + 1], func=ACT.Copy, scale=inv[:, t : t + 1])
 
         def shift_bus_plane():
-            nc.sync.dma_start(
+            nc.scalar.dma_start(
                 out=bus_picked_sc1[0:SHIFTED_ROWS, :].bitcast(I32),
                 in_=picked_sc["bus"][4 : 4 + SHIFTED_ROWS, :].bitcast(I32),
             )
 
         def round_line(c, a, *copies):
             line_bf[c, a] = kept([P, PACK, P, PACK], BF16, "line_bf%d%d" % (c, a))
-            share = P // RUN // len(copies)
-            for part, copy in enumerate(copies):
-                us = slice(share * part, share * (part + 1))
+            first = 0
+            for copy, share in copies:
+                ts = slice(first, first + share)
+                first = first + share
                 copy(
-                    out=line_bf[c, a][:].rearrange("p t (u e) i -> p u t i e", e=RUN)[:, us],
-                    in_=line_raw[c, a][:].rearrange("p i (u t e) -> p u t i e", t=PACK, e=RUN)[:, us],
+                    out=line_bf[c, a][:].rearrange("p t (u e) i -> p u t i e", e=RUN)[:, :, ts],
+                    in_=line_raw[c, a][:, :, :].rearrange("p i (u t e) -> p u t i e", t=PACK, e=RUN)[:, :, ts],
                 )
 
-        def round_state(c):
+        def round_state(c, *copies):
             state_bf[c] = kept([P, PACK, P, PACK], BF16, "state_bf%d" % c)
-            nc.scalar.copy(
-                out=state_bf[c][:].rearrange("p t m s -> p m s t"),
-                in_=state_raw[c][:].rearrange("p s (m t) -> p m s t", t=PACK),
-            )
+            first = 0
+            for copy, share in copies:
+                ms = slice(first, first + share)
+                first = first + share
+                copy(
+                    out=state_bf[c][:].rearrange("p t m s -> p m s t")[:, ms],
+                    in_=state_raw[c][:].rearrange("p s (m t) -> p m s t", t=PACK)[:, ms],
+                )
 
         def quantise(values, name):
             columns = values.shape[1] // PACK
@@ -149,7 +180,7 @@ def tile_list_grid_swing_flow_kernel(
 
         def adjacent(c, jt):
             js = slice(P * jt, P * (jt + 1))
-            adj = psum.tile([P, PASS], F32, tag="adj_or_flow", name="adj")
+            adj = banks[(4 * (2 * c + jt // 2)) % 6 + jt % 2]
             for a in range(PASSES):
                 nc.tensor.matmul_mx(
                     out=adj[:], lhsT=picked["adj", a][:, js].bitcast(FP8X4), lhsT_scale=picked_sc["adj"][4 * a :, js],
@@ -161,7 +192,7 @@ def tile_list_grid_swing_flow_kernel(
 
         def difference(c, jt):
             js = slice(P * jt, P * (jt + 1))
-            bus = psum.tile([P, PASS], F32, tag="bus_or_flow", name="bus")
+            bus = banks[(4 * (2 * c + jt // 2) + 2) % 6 + jt % 2]
             for a in range(PASSES):
                 nc.tensor.matmul_mx(
                     out=bus[:], lhsT=picked["bus", a][:, js].bitcast(FP8X4),
@@ -176,15 +207,15 @@ def tile_list_grid_swing_flow_kernel(
             )
 
         def sine(c, jt):
-            turned = psum.tile([P, PACK, P], F32, tag="turned", name="turned")
+            turned = by_group(banks[6 + jt % 2])
             for t in range(PACK):
                 nc.tensor.transpose(turned[:, t, :], diffs[c, jt][:, t, :], ident[:])
             sines[c, jt] = kept([P, P, PACK], F32, "sine%d%d" % (c, jt))
-            nc.scalar.activation(out=sines[c, jt][:], in_=turned[:].rearrange("p t j -> p j t"), func=ACT.Sin)
+            nc.scalar.activation(out=sines[c, jt][:], in_=turned.rearrange("p t j -> p j t"), func=ACT.Sin)
 
         def features(c, jt):
             js = slice(P * jt, P * (jt + 1))
-            line = psum.tile([P, PACK, P], F32, tag="line", name="line")
+            line = by_group(banks[(4, 5, 0, 1)[jt]])
             for t in range(PACK):
                 ms = slice(P * t, P * (t + 1))
                 for a in (1, 0):
@@ -195,7 +226,7 @@ def tile_list_grid_swing_flow_kernel(
                         start=(a == 1), stop=(a == 0),
                     )
             h_bf[c, jt] = h_first[:, js, :] if c == 0 else kept([P, P, PACK], BF16, "h_last%d" % jt)[:]
-            nc.vector.tensor_tensor(out=h_bf[c, jt], in0=line[:].rearrange("p t j -> p j t"), in1=sines[c, jt][:], op=ALU.mult)
+            nc.vector.tensor_tensor(out=h_bf[c, jt], in0=line.rearrange("p t j -> p j t"), in1=sines[c, jt][:], op=ALU.mult)
 
         def quantise_h_first():
             codes, plane = quantise(h_first[:].rearrange("p j t -> p (j t)"), "h_first")
@@ -206,114 +237,131 @@ def tile_list_grid_swing_flow_kernel(
             codes, plane = quantise(h_bf[1, jt].rearrange("p j t -> p (j t)"), "h_last%d" % jt)
             h_q[1, jt] = (codes[:], plane[:])
 
-        def project(jt):
-            banks = [psum.tile([P, 2, P], F32, tag=tag, name="flow") for tag in ("adj_or_flow", "bus_or_flow")]
+        def flow(c, jt):
+            if c == 0:
+                flows[jt] = by_group(banks[(2, 3, 6, 7)[jt]])
+            codes, plane = state_q[c]
             for t in range(PACK):
                 ms = slice(P * t, P * (t + 1))
-                for c in (1, 0):
-                    codes, plane = state_q[c]
-                    nc.tensor.matmul_mx(
-                        out=banks[t // 2][:, t % 2, :], lhsT=codes[:, ms].bitcast(FP8X4), lhsT_scale=plane[:, ms],
-                        rhs=h_q[c, jt][0].bitcast(FP8X4), rhs_scale=h_q[c, jt][1],
-                        start=(c == 1), stop=(c == 0),
-                    )
-            ys[jt] = kept([P, PACK, P], F32, "y%d" % jt)
+                nc.tensor.matmul_mx(
+                    out=flows[jt][:, t, :], lhsT=codes[:, ms].bitcast(FP8X4), lhsT_scale=plane[:, ms],
+                    rhs=h_q[c, jt][0].bitcast(FP8X4), rhs_scale=h_q[c, jt][1],
+                    start=(c == 0 and t == 0), stop=(c == PASSES - 1 and t == PACK - 1),
+                )
+
+        def project(jt):
+            ys[jt] = y_all[:, :, P * jt : P * (jt + 1)]
             for t in range(PACK):
                 nc.scalar.activation(
-                    out=ys[jt][:, t, :], in_=banks[t // 2][:, t % 2, :], func=ACT.Identity,
+                    out=ys[jt][:, t, :], in_=flows[jt][:, t, :], func=ACT.Identity,
                     bias=pin_inv[:, t : t + 1], scale=neg_inv[:, t : t + 1],
                 )
-            rows = out_0.rearrange("(p t) j -> p t j", t=PACK)
-            nc.sync.dma_start(out=rows[:, :, P * jt : P * (jt + 1)], in_=ys[jt][:])
+
+        def store_y(first, last):
+            js = slice(P * first, P * (last + 1))
+            nc.sync.dma_start(out=out_0.rearrange("(p t) j -> p t j", t=PACK)[:, :, js], in_=y_all[:, :, js])
+
+        def store_words(first, last, queue):
+            js = slice(P * first, P * (last + 1))
+            words_out = out_1[0].rearrange("p j t -> p (j t)").bitcast(I32)
+            queue.dma_start(out=words_out[:, js], in_=y_words[:, js].bitcast(I32))
 
         def planes(jt):
             js = slice(P * jt, P * (jt + 1))
             y_bf = kept([P, P, PACK], BF16, "y_bf%d" % jt)
             nc.vector.tensor_copy(
                 out=y_bf[:].rearrange("p (g e) t -> p g t e", e=RUN),
-                in_=ys[jt][:].rearrange("p t (g e) -> p g t e", e=RUN),
+                in_=ys[jt].rearrange("p t (g e) -> p g t e", e=RUN),
             )
             nc.vector.quantize_mx(out=y_words[:, js].bitcast(FP8X4), scales=y_sc[:, js], in_=y_bf[:].rearrange("p j t -> p (j t)"))
-            words_out = out_1[0].rearrange("p j t -> p (j t)").bitcast(I32)
-            queue = nc.scalar if jt == TILES - 1 else nc.sync
-            queue.dma_start(out=words_out[:, js], in_=y_words[:, js].bitcast(I32))
 
         on_scalar, on_vector = nc.scalar.copy, nc.vector.tensor_copy
 
-        nc.gpsimd.memset(tab_sc[:].bitcast(I32), 0)
-        nc.vector.memset(warm_in[:], 0.0)
-        nc.vector.memset(bus_picked_sc1[:].bitcast(I32), 0)
+        nc.vector.memset(tab_sc[:].bitcast(I32), 0)
         nc.vector.memset(adj_sc[:].bitcast(I32), 0)
+        nc.vector.memset(warm_in[:], 0.0)
         nc.vector.memset(bus_sc[:].bitcast(I32), 0)
-        nc.gpsimd.dma_start(out=pin[:], in_=pinj.rearrange("(p t) -> p t", t=PACK))
-        nc.gpsimd.dma_start(out=inv[:], in_=minv.rearrange("(p t) -> p t", t=PACK))
-        nc.gpsimd.tensor_scalar(out=neg_inv[:], in0=inv[:], scalar1=-1.0, scalar2=0.0, op0=ALU.mult, op1=ALU.add)
-        nc.gpsimd.tensor_tensor(out=pin_inv[:], in0=pin[:], in1=inv[:], op=ALU.mult)
+        nc.vector.memset(bus_picked_sc1[:].bitcast(I32), 0)
         make_identity(nc, ident[:])
         nc.scalar.activation(out=warm_out[:], in_=warm_in[:], func=ACT.Sin)
 
         load_list("bus", offs)
-        load_table_scales()
         load_list("adj", offs2)
+        load_table_scales()
+        load_weight_scales(adj_sc, wadj_scales, nc.scalar)
+        load_weight_scales(bus_sc, wbus_scales, nc.scalar)
         load_table(0)
         load_table(1)
-        gather_scales("bus")
-        load_adj(0)
-        shift_bus_plane()
         load_list("line", offs3)
-        load_adj(1)
+        load_adj(0)
         load_bus(0)
         load_line(0, 0)
-        load_bus(1)
         load_line(0, 1)
+        load_adj(1)
+        load_bus(1)
+        load_constants()
         load_line(1, 0)
-        load_state(0)
         load_line(1, 1)
+        load_state(0)
         load_state(1)
-        load_weight_scales(adj_sc, wadj_scales)
-        load_weight_scales(bus_sc, wbus_scales)
-
+        gather_scales("bus")
+        shift_bus_plane()
         gather_scales("adj")
-        for a in range(PASSES):
-            gather_words("adj", a)
-            gather_words("bus", a)
-        gather_scales("line")
-        for a in range(PASSES):
-            gather_words("line", a)
-
-        for jt in range(TILES):
-            adjacent(0, jt)
-        for jt in range(TILES):
-            difference(0, jt)
-        for jt in range(TILES):
-            adjacent(1, jt)
+        gather_words("adj", 0)
+        gather_words("bus", 0)
+        for half in range(2):
+            gather_words("adj", 1, half)
+            gather_words("bus", 1, half)
+        S1, V1, S2, V2 = (on_scalar, 1), (on_vector, 1), (on_scalar, 2), (on_vector, 2)
+        for pair in range(2):
+            for jt in (2 * pair, 2 * pair + 1):
+                adjacent(0, jt)
+            for jt in (2 * pair, 2 * pair + 1):
+                difference(0, jt)
         for jt in range(TILES):
             sine(0, jt)
-        round_line(0, 0, on_scalar)
-        round_line(0, 1, on_vector)
+        gather_scales("line")
+        gather_words("line", 0)
+        gather_words("line", 1)
+        round_line(0, 0, S1, S1, S1, S1)
         quantise_line(0, 0)
+        round_line(0, 1, V2, V2)
         quantise_line(0, 1)
-        for jt in range(TILES):
-            difference(1, jt)
-        for jt in range(TILES):
-            sine(1, jt)
-        round_state(0)
-        round_state(1)
-        round_line(1, 0, on_scalar, on_vector)
+        for pair in range(2):
+            for jt in (2 * pair, 2 * pair + 1):
+                adjacent(1, jt)
+            for jt in (2 * pair, 2 * pair + 1):
+                difference(1, jt)
+        for pair in range(2):
+            for jt in (2 * pair, 2 * pair + 1):
+                features(0, jt)
+            for jt in (2 * pair, 2 * pair + 1):
+                sine(1, jt)
+        round_line(1, 0, S1, S1, S1, S1)
         quantise_line(1, 0)
-        round_line(1, 1, on_vector)
+        round_line(1, 1, S1, S1, V2)
         quantise_line(1, 1)
+        round_state(0, (on_scalar, 32), (on_scalar, 32), (on_scalar, 32), (on_scalar, 32))
         quantise_state(0)
+        round_state(1, (on_scalar, 32), (on_scalar, 32), (on_vector, 64))
         quantise_state(1)
-        for jt in range(TILES):
-            features(0, jt)
         quantise_h_first()
+        for jt in range(TILES):
+            flow(0, jt)
         for jt in range(TILES):
             features(1, jt)
             quantise_h_last(jt)
+            flow(1, jt)
             project(jt)
-        for jt in range(TILES):
-            planes(jt)
+        store_y(0, 1)
+        planes(0)
+        planes(1)
+        store_y(2, 2)
+        planes(2)
+        store_words(0, 2, nc.sync)
+        store_y(3, 3)
+        planes(3)
+        store_words(3, 3, nc.scalar)
         for q in range(QUADS):
-            queue = nc.scalar if q == QUADS - 1 else nc.sync
+            queue = nc.scalar if q % 2 else nc.sync
             queue.dma_start(out=out_2[0, 4 * q : 4 * q + 4, :].bitcast(I32), in_=y_sc[32 * q : 32 * q + 4, :].bitcast(I32))

@@ -55,13 +55,16 @@ def tile_list_grid_swing_flow_kernel(
         inv = kept([P, PACK], F32, "inv")
         neg_inv = kept([P, PACK], F32, "neg_inv")
         pin_inv = kept([P, PACK], F32, "pin_inv")
-        h_first = kept([P, S, PACK], BF16, "h_first")
+        h_bf = [kept([P, S, PACK], BF16, "h_bf%d" % c) for c in range(PASSES)]
+        h_words = [kept([P, S], U32, "h_words%d" % c) for c in range(PASSES)]
+        h_sc = [kept([P, S], U8, "h_sc%d" % c) for c in range(PASSES)]
+        y_bf = kept([P, S, PACK], BF16, "y_bf")
         y_all = kept([P, PACK, S], F32, "y_all")
         y_words = kept([P, S], U32, "y_words")
         y_sc = kept([P, S], U8, "y_sc")
         lists, tab_w, adj_w, bus_w, line_raw, state_raw = {}, {}, {}, {}, {}, {}
         picked, picked_sc, line_bf, state_bf, line_q, state_q = {}, {}, {}, {}, {}, {}
-        adj_sb, diffs, sines, h_bf, h_q, ys, flows = {}, {}, {}, {}, {}, {}, {}
+        adj_sb, diffs, sines = {}, {}, {}
 
         def load_list(name, src):
             lists[name] = keep.tile([P, S // 16], U16, name="list_" + name)
@@ -225,55 +228,45 @@ def tile_list_grid_swing_flow_kernel(
                         rhs=picked["line", a][:, js].bitcast(FP8X4), rhs_scale=picked_sc["line"][4 * a :, js],
                         start=(a == 1), stop=(a == 0),
                     )
-            h_bf[c, jt] = h_first[:, js, :] if c == 0 else kept([P, P, PACK], BF16, "h_last%d" % jt)[:]
-            nc.vector.tensor_tensor(out=h_bf[c, jt], in0=line.rearrange("p t j -> p j t"), in1=sines[c, jt][:], op=ALU.mult)
+            nc.vector.tensor_tensor(out=h_bf[c][:, js, :], in0=line.rearrange("p t j -> p j t"), in1=sines[c, jt][:], op=ALU.mult)
 
-        def quantise_h_first():
-            codes, plane = quantise(h_first[:].rearrange("p j t -> p (j t)"), "h_first")
-            for jt in range(TILES):
-                h_q[0, jt] = (codes[:, P * jt : P * (jt + 1)], plane[:, P * jt : P * (jt + 1)])
+        def quantise_h(c, first, last):
+            js = slice(P * first, P * (last + 1))
+            nc.vector.quantize_mx(
+                out=h_words[c][:, js].bitcast(FP8X4), scales=h_sc[c][:, js], in_=h_bf[c][:, js, :].rearrange("p j t -> p (j t)"),
+            )
 
-        def quantise_h_last(jt):
-            codes, plane = quantise(h_bf[1, jt].rearrange("p j t -> p (j t)"), "h_last%d" % jt)
-            h_q[1, jt] = (codes[:], plane[:])
-
-        def flow(c, jt):
-            if c == 0:
-                flows[jt] = by_group(banks[(2, 3, 6, 7)[jt]])
+        def flow(c, t):
             codes, plane = state_q[c]
-            for t in range(PACK):
-                ms = slice(P * t, P * (t + 1))
-                nc.tensor.matmul_mx(
-                    out=flows[jt][:, t, :], lhsT=codes[:, ms].bitcast(FP8X4), lhsT_scale=plane[:, ms],
-                    rhs=h_q[c, jt][0].bitcast(FP8X4), rhs_scale=h_q[c, jt][1],
-                    start=(c == 0 and t == 0), stop=(c == PASSES - 1 and t == PACK - 1),
+            ms = slice(P * t, P * (t + 1))
+            nc.tensor.matmul_mx(
+                out=banks[(2, 3, 6, 7)[t]][:], lhsT=codes[:, ms].bitcast(FP8X4), lhsT_scale=plane[:, ms],
+                rhs=h_words[c][:].bitcast(FP8X4), rhs_scale=h_sc[c][:],
+                start=(c == 0), stop=(c == PASSES - 1),
+            )
+
+        def project(t):
+            bank, ts = banks[(2, 3, 6, 7)[t]], slice(t, t + 1)
+            if t % 2 == 0:
+                nc.scalar.activation(out=y_all[:, t, :], in_=bank[:], func=ACT.Identity, bias=pin_inv[:, ts], scale=neg_inv[:, ts])
+            else:
+                nc.vector.tensor_scalar(
+                    out=y_all[:, t, :], in0=bank[:], scalar1=neg_inv[:, ts], scalar2=pin_inv[:, ts], op0=ALU.mult, op1=ALU.add,
                 )
+            nc.sync.dma_start(out=out_0.rearrange("(p t) j -> p t j", t=PACK)[:, t, :], in_=y_all[:, t, :])
 
-        def project(jt):
-            ys[jt] = y_all[:, :, P * jt : P * (jt + 1)]
-            for t in range(PACK):
-                nc.scalar.activation(
-                    out=ys[jt][:, t, :], in_=flows[jt][:, t, :], func=ACT.Identity,
-                    bias=pin_inv[:, t : t + 1], scale=neg_inv[:, t : t + 1],
-                )
+        def round_y(first, last, copy):
+            gs = slice(P * first // RUN, P * (last + 1) // RUN)
+            copy(
+                out=y_bf[:].rearrange("p (g e) t -> p g t e", e=RUN)[:, gs],
+                in_=y_all[:].rearrange("p t (g e) -> p g t e", e=RUN)[:, gs],
+            )
 
-        def store_y(first, last):
+        def planes(first, last, queue):
             js = slice(P * first, P * (last + 1))
-            nc.sync.dma_start(out=out_0.rearrange("(p t) j -> p t j", t=PACK)[:, :, js], in_=y_all[:, :, js])
-
-        def store_words(first, last, queue):
-            js = slice(P * first, P * (last + 1))
+            nc.vector.quantize_mx(out=y_words[:, js].bitcast(FP8X4), scales=y_sc[:, js], in_=y_bf[:, js, :].rearrange("p j t -> p (j t)"))
             words_out = out_1[0].rearrange("p j t -> p (j t)").bitcast(I32)
             queue.dma_start(out=words_out[:, js], in_=y_words[:, js].bitcast(I32))
-
-        def planes(jt):
-            js = slice(P * jt, P * (jt + 1))
-            y_bf = kept([P, P, PACK], BF16, "y_bf%d" % jt)
-            nc.vector.tensor_copy(
-                out=y_bf[:].rearrange("p (g e) t -> p g t e", e=RUN),
-                in_=ys[jt].rearrange("p t (g e) -> p g t e", e=RUN),
-            )
-            nc.vector.quantize_mx(out=y_words[:, js].bitcast(FP8X4), scales=y_sc[:, js], in_=y_bf[:].rearrange("p j t -> p (j t)"))
 
         on_scalar, on_vector = nc.scalar.copy, nc.vector.tensor_copy
 
@@ -296,10 +289,9 @@ def tile_list_grid_swing_flow_kernel(
         load_adj(0)
         load_bus(0)
         load_line(0, 0)
-        load_line(0, 1)
         load_adj(1)
         load_bus(1)
-        load_constants()
+        load_line(0, 1)
         load_line(1, 0)
         load_line(1, 1)
         load_state(0)
@@ -313,55 +305,59 @@ def tile_list_grid_swing_flow_kernel(
             gather_words("adj", 1, half)
             gather_words("bus", 1, half)
         S1, V1, S2, V2 = (on_scalar, 1), (on_vector, 1), (on_scalar, 2), (on_vector, 2)
-        for pair in range(2):
-            for jt in (2 * pair, 2 * pair + 1):
-                adjacent(0, jt)
-            for jt in (2 * pair, 2 * pair + 1):
-                difference(0, jt)
-        for jt in range(TILES):
-            sine(0, jt)
+        def sums(c, jt):
+            adjacent(c, jt)
+            adjacent(c, jt + 1)
+            difference(c, jt)
+            difference(c, jt + 1)
+        def sines_of(c, jt):
+            sine(c, jt)
+            sine(c, jt + 1)
+        sums(0, 0)
+        sums(0, 2)
         gather_scales("line")
         gather_words("line", 0)
         gather_words("line", 1)
-        round_line(0, 0, S1, S1, S1, S1)
+        sines_of(0, 0)
+        sums(1, 0)
+        sines_of(0, 2)
+        round_line(0, 0, S1, S1, V2)
         quantise_line(0, 0)
         round_line(0, 1, V2, V2)
         quantise_line(0, 1)
-        for pair in range(2):
-            for jt in (2 * pair, 2 * pair + 1):
-                adjacent(1, jt)
-            for jt in (2 * pair, 2 * pair + 1):
-                difference(1, jt)
-        for pair in range(2):
-            for jt in (2 * pair, 2 * pair + 1):
-                features(0, jt)
-            for jt in (2 * pair, 2 * pair + 1):
-                sine(1, jt)
+        sums(1, 2)
         round_line(1, 0, S1, S1, S1, S1)
+        features(0, 0)
+        features(0, 1)
+        sines_of(1, 0)
+        round_line(1, 1, V2, V2)
         quantise_line(1, 0)
-        round_line(1, 1, S1, S1, V2)
         quantise_line(1, 1)
+        features(0, 2)
+        features(0, 3)
+        sines_of(1, 2)
         round_state(0, (on_scalar, 32), (on_scalar, 32), (on_scalar, 32), (on_scalar, 32))
+        load_constants()
+        round_state(1, (on_scalar, 32), (on_scalar, 32), (on_scalar, 32), (on_vector, 32))
+        features(1, 0)
+        features(1, 1)
+        quantise_h(0, 0, 3)
         quantise_state(0)
-        round_state(1, (on_scalar, 32), (on_scalar, 32), (on_vector, 64))
+        for t in range(PACK):
+            flow(0, t)
+        features(1, 2)
+        features(1, 3)
+        quantise_h(1, 0, 1)
         quantise_state(1)
-        quantise_h_first()
-        for jt in range(TILES):
-            flow(0, jt)
-        for jt in range(TILES):
-            features(1, jt)
-            quantise_h_last(jt)
-            flow(1, jt)
-            project(jt)
-        store_y(0, 1)
-        planes(0)
-        planes(1)
-        store_y(2, 2)
-        planes(2)
-        store_words(0, 2, nc.sync)
-        store_y(3, 3)
-        planes(3)
-        store_words(3, 3, nc.scalar)
+        quantise_h(1, 2, 3)
+        for t in range(PACK):
+            flow(1, t)
+            project(t)
+        round_y(0, 1, on_vector)
+        round_y(3, 3, on_scalar)
+        round_y(2, 2, on_vector)
+        planes(0, 1, nc.sync)
+        planes(2, 3, nc.scalar)
         for q in range(QUADS):
             queue = nc.scalar if q % 2 else nc.sync
             queue.dma_start(out=out_2[0, 4 * q : 4 * q + 4, :].bitcast(I32), in_=y_sc[32 * q : 32 * q + 4, :].bitcast(I32))

@@ -88,10 +88,17 @@ def tile_list_grid_swing_flow_kernel(
             tab_w[a] = kept([P, T], U32, "tab_w%d" % a)
             nc.sync.dma_start(out=tab_w[a][:].bitcast(I32), in_=tab_words[a].rearrange("p t i -> p (t i)").bitcast(I32))
 
-        def load_adj(c):
-            adj_w[c] = kept([P, PASSES, PASS], U32, "adj_w%d" % c)
+        def load_adj(c, a):
+            adj_w[c, a] = kept([P, PASS], U32, "adj_w%d%d" % (c, a))
+            words = wadj_words[a].rearrange("p c i -> p (c i)")
+            nc.sync.dma_start(out=adj_w[c, a][:].bitcast(I32), in_=words[:, 4 * PASS * c : 4 * PASS * (c + 1)].bitcast(I32))
+
+        def load_adj_both(c):
+            both = kept([P, PASSES, PASS], U32, "adj_w%d" % c)
             words = wadj_words.rearrange("a p c i -> p a (c i)")
-            nc.sync.dma_start(out=adj_w[c][:].bitcast(I32), in_=words[:, :, 4 * PASS * c : 4 * PASS * (c + 1)].bitcast(I32))
+            nc.sync.dma_start(out=both[:].bitcast(I32), in_=words[:, :, 4 * PASS * c : 4 * PASS * (c + 1)].bitcast(I32))
+            for a in range(PASSES):
+                adj_w[c, a] = both[:, a, :]
 
         def load_bus(c):
             bus_w[c] = kept([P, PASSES, 2 * PASS], U8, "bus_w%d" % c)
@@ -187,7 +194,7 @@ def tile_list_grid_swing_flow_kernel(
             for a in range(PASSES):
                 nc.tensor.matmul_mx(
                     out=adj[:], lhsT=picked["adj", a][:, js].bitcast(FP8X4), lhsT_scale=picked_sc["adj"][4 * a :, js],
-                    rhs=adj_w[c][:, a, :].bitcast(FP8X4), rhs_scale=adj_sc[:, a, PASS * c : PASS * (c + 1)],
+                    rhs=adj_w[c, a][:, :].bitcast(FP8X4), rhs_scale=adj_sc[:, a, PASS * c : PASS * (c + 1)],
                     start=(a == 0), stop=(a == PASSES - 1),
                 )
             adj_sb[c, jt] = kept([P, PACK, P], F32, "adj_sb%d%d" % (c, jt))
@@ -218,7 +225,7 @@ def tile_list_grid_swing_flow_kernel(
 
         def features(c, jt):
             js = slice(P * jt, P * (jt + 1))
-            line = by_group(banks[(4, 5, 0, 1)[jt]])
+            line = by_group(banks[((4, 5, 0, 1), (4, 5, 2, 3))[c][jt]])
             for t in range(PACK):
                 ms = slice(P * t, P * (t + 1))
                 for a in (1, 0):
@@ -240,13 +247,13 @@ def tile_list_grid_swing_flow_kernel(
             codes, plane = state_q[c]
             ms = slice(P * t, P * (t + 1))
             nc.tensor.matmul_mx(
-                out=banks[(2, 3, 6, 7)[t]][:], lhsT=codes[:, ms].bitcast(FP8X4), lhsT_scale=plane[:, ms],
+                out=banks[t][:], lhsT=codes[:, ms].bitcast(FP8X4), lhsT_scale=plane[:, ms],
                 rhs=h_words[c][:].bitcast(FP8X4), rhs_scale=h_sc[c][:],
                 start=(c == 0), stop=(c == PASSES - 1),
             )
 
         def project(t):
-            bank, ts = banks[(2, 3, 6, 7)[t]], slice(t, t + 1)
+            bank, ts = banks[t], slice(t, t + 1)
             if t % 2 == 0:
                 nc.scalar.activation(out=y_all[:, t, :], in_=bank[:], func=ACT.Identity, bias=pin_inv[:, ts], scale=neg_inv[:, ts])
             else:
@@ -268,6 +275,9 @@ def tile_list_grid_swing_flow_kernel(
             words_out = out_1[0].rearrange("p j t -> p (j t)").bitcast(I32)
             queue.dma_start(out=words_out[:, js], in_=y_words[:, js].bitcast(I32))
 
+        def on_gpsimd(out, in_):
+            nc.gpsimd.tensor_scalar(out=out, in0=in_, scalar1=1.0, scalar2=0.0, op0=ALU.mult, op1=ALU.add)
+
         on_scalar, on_vector = nc.scalar.copy, nc.vector.tensor_copy
 
         nc.vector.memset(tab_sc[:].bitcast(I32), 0)
@@ -286,12 +296,13 @@ def tile_list_grid_swing_flow_kernel(
         load_table(0)
         load_table(1)
         load_list("line", offs3)
-        load_adj(0)
+        load_adj_both(0)
         load_bus(0)
         load_line(0, 0)
-        load_adj(1)
+        load_adj_both(1)
         load_bus(1)
         load_line(0, 1)
+        load_constants()
         load_line(1, 0)
         load_line(1, 1)
         load_state(0)
@@ -313,6 +324,7 @@ def tile_list_grid_swing_flow_kernel(
         def sines_of(c, jt):
             sine(c, jt)
             sine(c, jt + 1)
+        G1 = (on_gpsimd, 1)
         sums(0, 0)
         sums(0, 2)
         gather_scales("line")
@@ -327,28 +339,28 @@ def tile_list_grid_swing_flow_kernel(
         quantise_line(0, 1)
         sums(1, 2)
         round_line(1, 0, S1, S1, S1, S1)
+        round_line(1, 1, V2, V2)
         features(0, 0)
         features(0, 1)
         sines_of(1, 0)
-        round_line(1, 1, V2, V2)
         quantise_line(1, 0)
         quantise_line(1, 1)
         features(0, 2)
         features(0, 3)
         sines_of(1, 2)
         round_state(0, (on_scalar, 32), (on_scalar, 32), (on_scalar, 32), (on_scalar, 32))
-        load_constants()
-        round_state(1, (on_scalar, 32), (on_scalar, 32), (on_scalar, 32), (on_vector, 32))
+
+        round_state(1, (on_scalar, 32), (on_scalar, 32), (on_scalar, 32), (on_scalar, 32))
         features(1, 0)
         features(1, 1)
         quantise_h(0, 0, 3)
         quantise_state(0)
+        quantise_h(1, 0, 1)
+        features(1, 2)
+        quantise_state(1)
+        features(1, 3)
         for t in range(PACK):
             flow(0, t)
-        features(1, 2)
-        features(1, 3)
-        quantise_h(1, 0, 1)
-        quantise_state(1)
         quantise_h(1, 2, 3)
         for t in range(PACK):
             flow(1, t)

@@ -104,6 +104,12 @@ def tile_list_grid_swing_flow_kernel(
             bus_w[c] = kept([P, PASSES, 2 * PASS], U8, "bus_w%d" % c)
             words = wbus_words.rearrange("a p c -> p a c")
             nc.sync.dma_start(out=bus_w[c][:].bitcast(I32), in_=words[:, :, 2 * PASS * c : 2 * PASS * (c + 1)].bitcast(I32))
+            for a in range(PASSES):
+                bus_w[c, a] = bus_w[c][:, a, :]
+
+        def load_bus_pass(c, a):
+            bus_w[c, a] = kept([P, 2 * PASS], U8, "bus_w%d%d" % (c, a))
+            nc.sync.dma_start(out=bus_w[c, a][:].bitcast(I32), in_=wbus_words[a][:, 2 * PASS * c : 2 * PASS * (c + 1)].bitcast(I32))
 
         def load_line(c, a):
             line_raw[c, a] = kept([P, PACK, PASS], F32, "line_raw%d%d" % (c, a))
@@ -172,6 +178,25 @@ def tile_list_grid_swing_flow_kernel(
                     in_=state_raw[c][:].rearrange("p s (m t) -> p m s t", t=PACK)[:, ms],
                 )
 
+        def round_state_pair(c, pair):
+            if c not in state_bf:
+                state_bf[c] = kept([P, PACK, P, PACK], BF16, "state_bf%d" % c)
+            ts = slice(2 * pair, 2 * pair + 2)
+            for ms in (slice(0, P // 2), slice(P // 2, P)):
+                nc.scalar.copy(
+                    out=state_bf[c][:].rearrange("p t m s -> p m s t")[:, ms, :, ts],
+                    in_=state_raw[c][:].rearrange("p s (m t) -> p m s t", t=PACK)[:, ms, :, ts],
+                )
+
+        def quantise_state_pair(c, pair):
+            if c not in state_q:
+                state_q[c] = (kept([P, N], U32, "state%d_words" % c), kept([P, N], U8, "state%d_sc" % c))
+            ms = slice(2 * P * pair, 2 * P * (pair + 1))
+            nc.vector.quantize_mx(
+                out=state_q[c][0][:, ms].bitcast(FP8X4), scales=state_q[c][1][:, ms],
+                in_=state_bf[c][:, 2 * pair : 2 * pair + 2].rearrange("p t m s -> p (t m s)"),
+            )
+
         def quantise(values, name):
             columns = values.shape[1] // PACK
             codes = kept([P, columns], U32, name + "_words")
@@ -207,7 +232,7 @@ def tile_list_grid_swing_flow_kernel(
                 nc.tensor.matmul_mx(
                     out=bus[:], lhsT=picked["bus", a][:, js].bitcast(FP8X4),
                     lhsT_scale=(picked_sc["bus"], bus_picked_sc1)[a][:, js],
-                    rhs=bus_w[c][:, a, :].bitcast(FP4X4), rhs_scale=bus_sc[:, a, PASS * c : PASS * (c + 1)],
+                    rhs=bus_w[c, a][:, :].bitcast(FP4X4), rhs_scale=bus_sc[:, a, PASS * c : PASS * (c + 1)],
                     start=(a == 0), stop=(a == PASSES - 1),
                 )
             diffs[c, jt] = kept([P, PACK, P], F32, "diff%d%d" % (c, jt))
@@ -281,8 +306,8 @@ def tile_list_grid_swing_flow_kernel(
         on_scalar, on_vector = nc.scalar.copy, nc.vector.tensor_copy
 
         nc.vector.memset(tab_sc[:].bitcast(I32), 0)
-        nc.vector.memset(adj_sc[:].bitcast(I32), 0)
         nc.vector.memset(warm_in[:], 0.0)
+        nc.vector.memset(adj_sc[:].bitcast(I32), 0)
         nc.vector.memset(bus_sc[:].bitcast(I32), 0)
         nc.vector.memset(bus_picked_sc1[:].bitcast(I32), 0)
         make_identity(nc, ident[:])
@@ -291,18 +316,17 @@ def tile_list_grid_swing_flow_kernel(
         load_list("bus", offs)
         load_list("adj", offs2)
         load_table_scales()
-        load_weight_scales(adj_sc, wadj_scales, nc.scalar)
-        load_weight_scales(bus_sc, wbus_scales, nc.scalar)
         load_table(0)
         load_table(1)
-        load_list("line", offs3)
+        load_weight_scales(adj_sc, wadj_scales, nc.sync)
         load_adj_both(0)
+        load_list("line", offs3)
+        load_weight_scales(bus_sc, wbus_scales, nc.sync)
         load_bus(0)
         load_line(0, 0)
         load_adj_both(1)
         load_bus(1)
         load_line(0, 1)
-        load_constants()
         load_line(1, 0)
         load_line(1, 1)
         load_state(0)
@@ -350,18 +374,21 @@ def tile_list_grid_swing_flow_kernel(
         sines_of(1, 2)
         round_state(0, (on_scalar, 32), (on_scalar, 32), (on_scalar, 32), (on_scalar, 32))
 
-        round_state(1, (on_scalar, 32), (on_scalar, 32), (on_scalar, 32), (on_scalar, 32))
+        load_constants()
+        round_state_pair(1, 0)
+        round_state_pair(1, 1)
         features(1, 0)
         features(1, 1)
         quantise_h(0, 0, 3)
         quantise_state(0)
         quantise_h(1, 0, 1)
         features(1, 2)
-        quantise_state(1)
+        quantise_state_pair(1, 0)
         features(1, 3)
         for t in range(PACK):
             flow(0, t)
         quantise_h(1, 2, 3)
+        quantise_state_pair(1, 1)
         for t in range(PACK):
             flow(1, t)
             project(t)

@@ -213,6 +213,9 @@ def tile_list_grid_swing_flow_kernel(
         def by_slot(ap):
             return ap.rearrange("j (u t e) -> j t u e", t=PACK, e=RUN)
 
+        def by_pair(bank):
+            return bank.rearrange("p t (g e) -> p g t e", e=2)
+
         def adjacent(c, jt):
             js = slice(P * jt, P * (jt + 1))
             adj = banks[(4 * (2 * c + jt // 2)) % 6 + jt % 2]
@@ -245,8 +248,8 @@ def tile_list_grid_swing_flow_kernel(
             turned = by_group(banks[6 + jt % 2])
             for t in range(PACK):
                 nc.tensor.transpose(turned[:, t, :], diffs[c, jt][:, t, :], ident[:])
-            sines[c, jt] = kept([P, P, PACK], F32, "sine%d%d" % (c, jt))
-            nc.scalar.activation(out=sines[c, jt][:], in_=turned.rearrange("p t j -> p j t"), func=ACT.Sin)
+            sines[c, jt] = kept([P, P // 2, PACK, 2], F32, "sine%d%d" % (c, jt))
+            nc.scalar.activation(out=sines[c, jt][:], in_=by_pair(turned), func=ACT.Sin)
 
         def features(c, jt):
             js = slice(P * jt, P * (jt + 1))
@@ -260,7 +263,9 @@ def tile_list_grid_swing_flow_kernel(
                         rhs=picked["line", a][:, js].bitcast(FP8X4), rhs_scale=picked_sc["line"][4 * a :, js],
                         start=(a == 1), stop=(a == 0),
                     )
-            nc.vector.tensor_tensor(out=h_bf[c][:, js, :], in0=line.rearrange("p t j -> p j t"), in1=sines[c, jt][:], op=ALU.mult)
+            nc.vector.tensor_tensor(
+                out=h_bf[c][:, js, :].rearrange("p (g e) t -> p g t e", e=2), in0=by_pair(line), in1=sines[c, jt][:], op=ALU.mult,
+            )
 
         def quantise_h(c, first, last):
             js = slice(P * first, P * (last + 1))

@@ -25,6 +25,12 @@ QUADS = 4
 TILES = S // P
 RUN = 4
 SHIFTED_ROWS = 100
+QUARTER = P // 4
+Y_ON_VECTOR = 336
+
+SUM_BANKS = 6
+TURN_BANK = 6
+LINE_BANK = (4, 0, 4, 2)
 
 
 def tile_list_grid_swing_flow_kernel(
@@ -35,11 +41,7 @@ def tile_list_grid_swing_flow_kernel(
     with ExitStack() as ctx:
         keep = ctx.enter_context(tc.tile_pool(name="keep", bufs=1))
         psum = ctx.enter_context(tc.psum_pool(name="psum", bufs=1))
-
         banks = [psum.tile([P, PASS], F32, name="bank%d" % b) for b in range(8)]
-
-        def by_group(bank):
-            return bank[:].rearrange("p (t j) -> p t j", t=PACK)
 
         def kept(shape, dtype, name):
             return keep.tile(shape, dtype, name=name, align_bytes=64)
@@ -48,8 +50,8 @@ def tile_list_grid_swing_flow_kernel(
         adj_sc = kept([P, PASSES, H], U8, "adj_sc")
         bus_sc = kept([P, PASSES, H], U8, "bus_sc")
         bus_picked_sc1 = kept([P, S], U8, "bus_picked_sc1")
-        warm_in = kept([P, 1], F32, "warm_in")
-        warm_out = kept([P, 1], F32, "warm_out")
+        angle0 = kept([P, 1], F32, "angle0")
+        zero = kept([P, 1], F32, "zero")
         ident = kept([P, P], F32, "ident")
         pin = kept([P, PACK], F32, "pin")
         inv = kept([P, PACK], F32, "inv")
@@ -58,13 +60,17 @@ def tile_list_grid_swing_flow_kernel(
         h_bf = [kept([P, S, PACK], BF16, "h_bf%d" % c) for c in range(PASSES)]
         h_words = [kept([P, S], U32, "h_words%d" % c) for c in range(PASSES)]
         h_sc = [kept([P, S], U8, "h_sc%d" % c) for c in range(PASSES)]
+        state_bf = [kept([P, PACK, P, PACK], BF16, "state_bf%d" % c) for c in range(PASSES)]
+        state_words = [kept([P, N], U32, "state_words%d" % c) for c in range(PASSES)]
+        state_sc = [kept([P, N], U8, "state_sc%d" % c) for c in range(PASSES)]
+        y = kept([P, PACK, S], F32, "y")
         y_bf = kept([P, S, PACK], BF16, "y_bf")
-        y_all = kept([P, PACK, S], F32, "y_all")
         y_words = kept([P, S], U32, "y_words")
         y_sc = kept([P, S], U8, "y_sc")
         lists, tab_w, adj_w, bus_w, line_raw, state_raw = {}, {}, {}, {}, {}, {}
-        picked, picked_sc, line_bf, state_bf, line_q, state_q = {}, {}, {}, {}, {}, {}
+        picked, picked_sc, line_bf, line_q = {}, {}, {}, {}
         adj_sb, diffs, sines = {}, {}, {}
+        on_scalar, on_vector = nc.scalar.copy, nc.vector.tensor_copy
 
         def load_list(name, src):
             lists[name] = keep.tile([P, S // 16], U16, name="list_" + name)
@@ -77,9 +83,9 @@ def tile_list_grid_swing_flow_kernel(
                     in_=tab_scales[:, 4 * q : 4 * q + 4, :].bitcast(I32),
                 )
 
-        def load_weight_scales(planes, scales, queue):
+        def load_weight_scales(planes, scales):
             for q in range(QUADS):
-                queue.dma_start(
+                nc.sync.dma_start(
                     out=planes[32 * q : 32 * q + 4, :, :].bitcast(I32),
                     in_=scales[:, 4 * q : 4 * q + 4, :].rearrange("a r c -> r a c").bitcast(I32),
                 )
@@ -88,67 +94,42 @@ def tile_list_grid_swing_flow_kernel(
             tab_w[a] = kept([P, T], U32, "tab_w%d" % a)
             nc.sync.dma_start(out=tab_w[a][:].bitcast(I32), in_=tab_words[a].rearrange("p t i -> p (t i)").bitcast(I32))
 
-        def load_adj(c, a):
-            adj_w[c, a] = kept([P, PASS], U32, "adj_w%d%d" % (c, a))
-            words = wadj_words[a].rearrange("p c i -> p (c i)")
-            nc.sync.dma_start(out=adj_w[c, a][:].bitcast(I32), in_=words[:, 4 * PASS * c : 4 * PASS * (c + 1)].bitcast(I32))
-
-        def load_adj_both(c):
-            both = kept([P, PASSES, PASS], U32, "adj_w%d" % c)
+        def load_adj(c):
+            adj_w[c] = kept([P, PASSES, PASS], U32, "adj_w%d" % c)
             words = wadj_words.rearrange("a p c i -> p a (c i)")
-            nc.sync.dma_start(out=both[:].bitcast(I32), in_=words[:, :, 4 * PASS * c : 4 * PASS * (c + 1)].bitcast(I32))
-            for a in range(PASSES):
-                adj_w[c, a] = both[:, a, :]
+            nc.sync.dma_start(out=adj_w[c][:].bitcast(I32), in_=words[:, :, 4 * PASS * c : 4 * PASS * (c + 1)].bitcast(I32))
 
         def load_bus(c):
             bus_w[c] = kept([P, PASSES, 2 * PASS], U8, "bus_w%d" % c)
             words = wbus_words.rearrange("a p c -> p a c")
             nc.sync.dma_start(out=bus_w[c][:].bitcast(I32), in_=words[:, :, 2 * PASS * c : 2 * PASS * (c + 1)].bitcast(I32))
-            for a in range(PASSES):
-                bus_w[c, a] = bus_w[c][:, a, :]
-
-        def load_bus_pass(c, a):
-            bus_w[c, a] = kept([P, 2 * PASS], U8, "bus_w%d%d" % (c, a))
-            nc.sync.dma_start(out=bus_w[c, a][:].bitcast(I32), in_=wbus_words[a][:, 2 * PASS * c : 2 * PASS * (c + 1)].bitcast(I32))
 
         def load_line(c, a):
             line_raw[c, a] = kept([P, PACK, PASS], F32, "line_raw%d%d" % (c, a))
             rows = wline[PASS * a : PASS * (a + 1), PASS * c : PASS * (c + 1)]
             nc.sync.dma_start(out=line_raw[c, a][:], in_=rows.rearrange("(p i) r -> p i r", i=PACK))
 
-        def load_line_pass(a):
-            both = kept([P, PACK, H], F32, "line_raw%d" % a)
-            nc.sync.dma_start(out=both[:], in_=wline[PASS * a : PASS * (a + 1), :].rearrange("(p i) r -> p i r", i=PACK))
-            for c in range(PASSES):
-                line_raw[c, a] = both[:, :, PASS * c : PASS * (c + 1)]
-
         def load_state(c):
             state_raw[c] = kept([P, PACK, N], F32, "state_raw%d" % c)
-            rows = wstate[PASS * c : PASS * (c + 1), :].rearrange("(u t e) n -> t u e n", t=PACK, e=RUN)
+            rows = wstate[PASS * c : PASS * (c + 1), :]
+            nc.sync.dma_start(out=state_raw[c][:], in_=rows.rearrange("(p t) n -> p t n", t=PACK))
+
+        def constants():
+            nc.sync.dma_start(out=pin[:], in_=pinj.rearrange("(p t) -> p t", t=PACK))
+            nc.sync.dma_start(out=inv[:], in_=minv.rearrange("(p t) -> p t", t=PACK))
+            nc.scalar.activation(out=neg_inv[:], in_=inv[:], func=ACT.Identity, bias=zero[:], scale=-1.0)
             for t in range(PACK):
-                nc.sync.dma_start(out=state_raw[c][:, t, :], in_=rows[t])
+                nc.scalar.activation(out=pin_inv[:, t : t + 1], in_=pin[:, t : t + 1], func=ACT.Copy, scale=inv[:, t : t + 1])
 
         def gather_scales(name):
             picked_sc[name] = kept([P, S], U8, "picked_sc_" + name)
             nc.vector.tensor_copy(picked_sc[name][:], tab_sc[:].indirect(lists[name][:]))
 
-        def gather_words(name, a, half=None):
-            if (name, a) not in picked:
+        def gather_words(name, a, first, last):
+            if first == 0:
                 picked[name, a] = kept([P, S], U32, "picked_%s%d" % (name, a))
-            if half is None:
-                nc.vector.tensor_copy(picked[name, a][:], tab_w[a][:].indirect(lists[name][:]))
-            else:
-                nc.vector.tensor_copy(
-                    picked[name, a][:, S // 2 * half : S // 2 * (half + 1)],
-                    tab_w[a][:].indirect(lists[name][:, S // 32 * half : S // 32 * (half + 1)]),
-                )
-
-        def load_constants():
-            nc.sync.dma_start(out=pin[:], in_=pinj.rearrange("(p t) -> p t", t=PACK))
-            nc.sync.dma_start(out=inv[:], in_=minv.rearrange("(p t) -> p t", t=PACK))
-            nc.scalar.activation(out=neg_inv[:], in_=inv[:], func=ACT.Copy, scale=-1.0)
-            for t in range(PACK):
-                nc.scalar.activation(out=pin_inv[:, t : t + 1], in_=pin[:, t : t + 1], func=ACT.Copy, scale=inv[:, t : t + 1])
+            offsets = lists[name][:, P // 16 * first : P // 16 * (last + 1)]
+            nc.vector.tensor_copy(picked[name, a][:, P * first : P * (last + 1)], tab_w[a][:].indirect(offsets))
 
         def shift_bus_plane():
             nc.scalar.dma_start(
@@ -156,219 +137,184 @@ def tile_list_grid_swing_flow_kernel(
                 in_=picked_sc["bus"][4 : 4 + SHIFTED_ROWS, :].bitcast(I32),
             )
 
-        def round_line(c, a, *copies):
-            line_bf[c, a] = kept([P, PACK, P, PACK], BF16, "line_bf%d%d" % (c, a))
-            first = 0
-            for copy, share in copies:
-                ts = slice(first, first + share)
-                first = first + share
-                copy(
-                    out=line_bf[c, a][:].rearrange("p t (u e) i -> p u t i e", e=RUN)[:, :, ts],
-                    in_=line_raw[c, a][:, :, :].rearrange("p i (u t e) -> p u t i e", t=PACK, e=RUN)[:, :, ts],
-                )
-
-        def round_state(c, *copies):
-            state_bf[c] = kept([P, PACK, P, PACK], BF16, "state_bf%d" % c)
-            first = 0
-            for copy, share in copies:
-                ms = slice(first, first + share)
-                first = first + share
-                copy(
-                    out=state_bf[c][:].rearrange("p t m s -> p m s t")[:, ms],
-                    in_=state_raw[c][:].rearrange("p s (m t) -> p m s t", t=PACK)[:, ms],
-                )
-
-        def round_state_pair(c, pair):
-            if c not in state_bf:
-                state_bf[c] = kept([P, PACK, P, PACK], BF16, "state_bf%d" % c)
-            ts = slice(2 * pair, 2 * pair + 2)
-            for ms in (slice(0, P // 2), slice(P // 2, P)):
-                nc.scalar.copy(
-                    out=state_bf[c][:].rearrange("p t m s -> p m s t")[:, ms, :, ts],
-                    in_=state_raw[c][:].rearrange("p s (m t) -> p m s t", t=PACK)[:, ms, :, ts],
-                )
-
-        def quantise_state_pair(c, pair):
-            if c not in state_q:
-                state_q[c] = (kept([P, N], U32, "state%d_words" % c), kept([P, N], U8, "state%d_sc" % c))
-            ms = slice(2 * P * pair, 2 * P * (pair + 1))
-            nc.vector.quantize_mx(
-                out=state_q[c][0][:, ms].bitcast(FP8X4), scales=state_q[c][1][:, ms],
-                in_=state_bf[c][:, 2 * pair : 2 * pair + 2].rearrange("p t m s -> p (t m s)"),
+        def deal(copy, rounded, raw, quarter, quarters, slots):
+            ms = slice(QUARTER * quarter, QUARTER * (quarter + quarters))
+            copy(
+                out=rounded[:].rearrange("p t m i -> p m i t")[:, ms, :, slots],
+                in_=raw[:].rearrange("p i (m t) -> p m i t", t=PACK)[:, ms, :, slots],
             )
 
-        def quantise(values, name):
-            columns = values.shape[1] // PACK
-            codes = kept([P, columns], U32, name + "_words")
-            plane = kept([P, columns], U8, name + "_sc")
-            nc.vector.quantize_mx(out=codes[:].bitcast(FP8X4), scales=plane[:], in_=values)
-            return codes, plane
+        def round_line(c, a, scalar_quarters):
+            line_bf[c, a] = kept([P, PACK, P, PACK], BF16, "line_bf%d%d" % (c, a))
+            for quarter in range(scalar_quarters):
+                deal(on_scalar, line_bf[c, a], line_raw[c, a], quarter, 1, slice(0, PACK))
+            for quarter in range(scalar_quarters, 4, 2):
+                deal(on_vector, line_bf[c, a], line_raw[c, a], quarter, 2, slice(0, PACK))
+
+        def quantise(words, plane, values):
+            nc.vector.quantize_mx(out=words.bitcast(FP8X4), scales=plane, in_=values)
 
         def quantise_line(c, a):
-            line_q[c, a] = quantise(line_bf[c, a][:].rearrange("p t m i -> p (t m i)"), "line%d%d" % (c, a))
+            line_q[c, a] = (kept([P, PASS], U32, "line_words%d%d" % (c, a)), kept([P, PASS], U8, "line_sc%d%d" % (c, a)))
+            quantise(line_q[c, a][0][:], line_q[c, a][1][:], line_bf[c, a][:].rearrange("p t m i -> p (t m i)"))
 
-        def quantise_state(c):
-            state_q[c] = quantise(state_bf[c][:].rearrange("p t m s -> p (t m s)"), "state%d" % c)
+        def quantise_state(c, first, last):
+            ms = slice(P * first, P * (last + 1))
+            quantise(state_words[c][:, ms], state_sc[c][:, ms], state_bf[c][:, first : last + 1].rearrange("p t m i -> p (t m i)"))
 
-        def by_slot(ap):
-            return ap.rearrange("j (u t e) -> j t u e", t=PACK, e=RUN)
+        def by_slot(bank):
+            return bank[:].rearrange("j (m t) -> j t m", t=PACK)
 
-        def by_pair(bank):
-            return bank.rearrange("p t (g e) -> p g t e", e=2)
+        def by_group(bank):
+            return bank[:].rearrange("p (t j) -> p t j", t=PACK)
+
+        def by_two(bank):
+            return bank[:].rearrange("p (t g e) -> p g t e", t=PACK, e=2)
 
         def adjacent(c, jt):
             js = slice(P * jt, P * (jt + 1))
-            adj = banks[(4 * (2 * c + jt // 2)) % 6 + jt % 2]
+            adj = banks[4 * (2 * c + jt // 2) % SUM_BANKS + jt % 2]
             for a in range(PASSES):
                 nc.tensor.matmul_mx(
                     out=adj[:], lhsT=picked["adj", a][:, js].bitcast(FP8X4), lhsT_scale=picked_sc["adj"][4 * a :, js],
-                    rhs=adj_w[c, a][:, :].bitcast(FP8X4), rhs_scale=adj_sc[:, a, PASS * c : PASS * (c + 1)],
+                    rhs=adj_w[c][:, a, :].bitcast(FP8X4), rhs_scale=adj_sc[:, a, PASS * c : PASS * (c + 1)],
                     start=(a == 0), stop=(a == PASSES - 1),
                 )
             adj_sb[c, jt] = kept([P, PACK, P], F32, "adj_sb%d%d" % (c, jt))
-            nc.scalar.copy(out=adj_sb[c, jt][:].rearrange("j t (u e) -> j t u e", e=RUN), in_=by_slot(adj[:]))
+            nc.scalar.copy(out=adj_sb[c, jt][:], in_=by_slot(adj))
 
         def difference(c, jt):
             js = slice(P * jt, P * (jt + 1))
-            bus = banks[(4 * (2 * c + jt // 2) + 2) % 6 + jt % 2]
+            bus = banks[(4 * (2 * c + jt // 2) + 2) % SUM_BANKS + jt % 2]
             for a in range(PASSES):
                 nc.tensor.matmul_mx(
                     out=bus[:], lhsT=picked["bus", a][:, js].bitcast(FP8X4),
                     lhsT_scale=(picked_sc["bus"], bus_picked_sc1)[a][:, js],
-                    rhs=bus_w[c, a][:, :].bitcast(FP4X4), rhs_scale=bus_sc[:, a, PASS * c : PASS * (c + 1)],
+                    rhs=bus_w[c][:, a, :].bitcast(FP4X4), rhs_scale=bus_sc[:, a, PASS * c : PASS * (c + 1)],
                     start=(a == 0), stop=(a == PASSES - 1),
                 )
             diffs[c, jt] = kept([P, PACK, P], F32, "diff%d%d" % (c, jt))
-            nc.vector.tensor_tensor(
-                out=diffs[c, jt][:].rearrange("j t (u e) -> j t u e", e=RUN), in0=by_slot(bus[:]),
-                in1=adj_sb[c, jt][:].rearrange("j t (u e) -> j t u e", e=RUN), op=ALU.subtract,
-            )
+            nc.vector.tensor_tensor(out=diffs[c, jt][:], in0=by_slot(bus), in1=adj_sb[c, jt][:], op=ALU.subtract)
 
         def sine(c, jt):
-            turned = by_group(banks[6 + jt % 2])
+            turned = banks[TURN_BANK + jt % 2]
             for t in range(PACK):
-                nc.tensor.transpose(turned[:, t, :], diffs[c, jt][:, t, :], ident[:])
+                nc.tensor.transpose(by_group(turned)[:, t, :], diffs[c, jt][:, t, :], ident[:])
             sines[c, jt] = kept([P, P // 2, PACK, 2], F32, "sine%d%d" % (c, jt))
-            nc.scalar.activation(out=sines[c, jt][:], in_=by_pair(turned), func=ACT.Sin)
+            nc.scalar.activation(out=sines[c, jt][:], in_=by_two(turned), func=ACT.Sin)
 
         def features(c, jt):
             js = slice(P * jt, P * (jt + 1))
-            line = by_group(banks[((4, 5, 0, 1), (4, 5, 2, 3))[c][jt]])
+            line = banks[LINE_BANK[2 * c + jt // 2] + jt % 2]
             for t in range(PACK):
                 ms = slice(P * t, P * (t + 1))
                 for a in (1, 0):
-                    codes, plane = line_q[c, a]
+                    words, plane = line_q[c, a]
                     nc.tensor.matmul_mx(
-                        out=line[:, t, :], lhsT=codes[:, ms].bitcast(FP8X4), lhsT_scale=plane[:, ms],
+                        out=by_group(line)[:, t, :], lhsT=words[:, ms].bitcast(FP8X4), lhsT_scale=plane[:, ms],
                         rhs=picked["line", a][:, js].bitcast(FP8X4), rhs_scale=picked_sc["line"][4 * a :, js],
                         start=(a == 1), stop=(a == 0),
                     )
             nc.vector.tensor_tensor(
-                out=h_bf[c][:, js, :].rearrange("p (g e) t -> p g t e", e=2), in0=by_pair(line), in1=sines[c, jt][:], op=ALU.mult,
+                out=h_bf[c][:, js, :].rearrange("p (g e) t -> p g t e", e=2), in0=by_two(line), in1=sines[c, jt][:], op=ALU.mult,
             )
+
+        def sums(c, jt):
+            adjacent(c, jt)
+            adjacent(c, jt + 1)
+            difference(c, jt)
+            difference(c, jt + 1)
+
+        def sines_of(c, jt):
+            sine(c, jt)
+            sine(c, jt + 1)
 
         def quantise_h(c, first, last):
             js = slice(P * first, P * (last + 1))
-            nc.vector.quantize_mx(
-                out=h_words[c][:, js].bitcast(FP8X4), scales=h_sc[c][:, js], in_=h_bf[c][:, js, :].rearrange("p j t -> p (j t)"),
-            )
+            quantise(h_words[c][:, js], h_sc[c][:, js], h_bf[c][:, js, :].rearrange("p j t -> p (j t)"))
 
         def flow(c, t):
-            codes, plane = state_q[c]
             ms = slice(P * t, P * (t + 1))
             nc.tensor.matmul_mx(
-                out=banks[t][:], lhsT=codes[:, ms].bitcast(FP8X4), lhsT_scale=plane[:, ms],
+                out=banks[t][:], lhsT=state_words[c][:, ms].bitcast(FP8X4), lhsT_scale=state_sc[c][:, ms],
                 rhs=h_words[c][:].bitcast(FP8X4), rhs_scale=h_sc[c][:],
                 start=(c == 0), stop=(c == PASSES - 1),
             )
 
         def project(t):
-            bank, ts = banks[t], slice(t, t + 1)
+            ts = slice(t, t + 1)
             if t % 2 == 0:
-                nc.scalar.activation(out=y_all[:, t, :], in_=bank[:], func=ACT.Identity, bias=pin_inv[:, ts], scale=neg_inv[:, ts])
+                nc.scalar.activation(out=y[:, t, :], in_=banks[t][:], func=ACT.Identity, bias=pin_inv[:, ts], scale=neg_inv[:, ts])
             else:
                 nc.vector.tensor_scalar(
-                    out=y_all[:, t, :], in0=bank[:], scalar1=neg_inv[:, ts], scalar2=pin_inv[:, ts], op0=ALU.mult, op1=ALU.add,
+                    out=y[:, t, :], in0=banks[t][:], scalar1=neg_inv[:, ts], scalar2=pin_inv[:, ts], op0=ALU.mult, op1=ALU.add,
                 )
-            nc.sync.dma_start(out=out_0.rearrange("(p t) j -> p t j", t=PACK)[:, t, :], in_=y_all[:, t, :])
+            nc.sync.dma_start(out=out_0.rearrange("(p t) j -> p t j", t=PACK)[:, t, :], in_=y[:, t, :])
 
-        def round_y(first, last, copy):
-            gs = slice(P * first // RUN, P * (last + 1) // RUN)
+        def round_y(copy, first, end):
+            gs = slice(first // RUN, end // RUN)
             copy(
                 out=y_bf[:].rearrange("p (g e) t -> p g t e", e=RUN)[:, gs],
-                in_=y_all[:].rearrange("p t (g e) -> p g t e", e=RUN)[:, gs],
+                in_=y[:].rearrange("p t (g e) -> p g t e", e=RUN)[:, gs],
             )
 
-        def planes(first, last, queue):
-            js = slice(P * first, P * (last + 1))
-            nc.vector.quantize_mx(out=y_words[:, js].bitcast(FP8X4), scales=y_sc[:, js], in_=y_bf[:, js, :].rearrange("p j t -> p (j t)"))
+        def planes(half, queue):
+            js = slice(S // 2 * half, S // 2 * (half + 1))
+            quantise(y_words[:, js], y_sc[:, js], y_bf[:, js, :].rearrange("p j t -> p (j t)"))
             words_out = out_1[0].rearrange("p j t -> p (j t)").bitcast(I32)
             queue.dma_start(out=words_out[:, js], in_=y_words[:, js].bitcast(I32))
 
-        def on_gpsimd(out, in_):
-            nc.gpsimd.tensor_scalar(out=out, in0=in_, scalar1=1.0, scalar2=0.0, op0=ALU.mult, op1=ALU.add)
-
-        on_scalar, on_vector = nc.scalar.copy, nc.vector.tensor_copy
-
         nc.vector.memset(tab_sc[:].bitcast(I32), 0)
-        nc.vector.memset(warm_in[:], 0.0)
+        nc.vector.memset(angle0[:], 0.0)
         nc.vector.memset(adj_sc[:].bitcast(I32), 0)
         nc.vector.memset(bus_sc[:].bitcast(I32), 0)
         nc.vector.memset(bus_picked_sc1[:].bitcast(I32), 0)
         make_identity(nc, ident[:])
-        nc.scalar.activation(out=warm_out[:], in_=warm_in[:], func=ACT.Sin)
+        nc.scalar.activation(out=zero[:], in_=angle0[:], func=ACT.Sin)
 
         load_list("bus", offs)
         load_list("adj", offs2)
         load_table_scales()
         load_table(0)
         load_table(1)
-        load_weight_scales(adj_sc, wadj_scales, nc.sync)
-        load_adj_both(0)
+        load_weight_scales(adj_sc, wadj_scales)
+        load_adj(0)
         load_list("line", offs3)
-        load_weight_scales(bus_sc, wbus_scales, nc.sync)
+        load_weight_scales(bus_sc, wbus_scales)
         load_bus(0)
         load_line(0, 0)
-        load_adj_both(1)
+        load_adj(1)
         load_bus(1)
         load_line(0, 1)
         load_line(1, 0)
         load_line(1, 1)
         load_state(0)
         load_state(1)
+
         gather_scales("bus")
         shift_bus_plane()
         gather_scales("adj")
-        gather_words("adj", 0)
-        gather_words("bus", 0)
-        for half in range(2):
-            gather_words("adj", 1, half)
-            gather_words("bus", 1, half)
-        S1, V1, S2, V2 = (on_scalar, 1), (on_vector, 1), (on_scalar, 2), (on_vector, 2)
-        def sums(c, jt):
-            adjacent(c, jt)
-            adjacent(c, jt + 1)
-            difference(c, jt)
-            difference(c, jt + 1)
-        def sines_of(c, jt):
-            sine(c, jt)
-            sine(c, jt + 1)
-        G1 = (on_gpsimd, 1)
+        gather_words("adj", 0, 0, TILES - 1)
+        gather_words("bus", 0, 0, TILES - 1)
+        for first in (0, 2):
+            gather_words("adj", 1, first, first + 1)
+            gather_words("bus", 1, first, first + 1)
+
         sums(0, 0)
         sums(0, 2)
         gather_scales("line")
-        gather_words("line", 0)
-        gather_words("line", 1)
+        for a in range(PASSES):
+            gather_words("line", a, 0, TILES - 1)
         sines_of(0, 0)
         sums(1, 0)
         sines_of(0, 2)
-        round_line(0, 0, S1, S1, V2)
+        round_line(0, 0, 2)
         quantise_line(0, 0)
-        round_line(0, 1, V2, V2)
+        round_line(0, 1, 0)
         quantise_line(0, 1)
         sums(1, 2)
-        round_line(1, 0, S1, S1, S1, S1)
-        round_line(1, 1, V2, V2)
+        round_line(1, 0, 4)
+        round_line(1, 1, 2)
         features(0, 0)
         features(0, 1)
         sines_of(1, 0)
@@ -377,31 +323,32 @@ def tile_list_grid_swing_flow_kernel(
         features(0, 2)
         features(0, 3)
         sines_of(1, 2)
-        round_state(0, (on_scalar, 32), (on_scalar, 32), (on_scalar, 32), (on_scalar, 32))
-
-        load_constants()
-        round_state_pair(1, 0)
-        round_state_pair(1, 1)
+        for quarter in range(4):
+            deal(on_scalar, state_bf[0], state_raw[0], quarter, 1, slice(0, PACK))
+        constants()
+        for copy, slots in ((on_scalar, slice(0, 2)), (on_vector, slice(2, PACK))):
+            for quarter in (0, 2):
+                deal(copy, state_bf[1], state_raw[1], quarter, 2, slots)
         features(1, 0)
         features(1, 1)
-        quantise_h(0, 0, 3)
-        quantise_state(0)
+        quantise_h(0, 0, TILES - 1)
+        quantise_state(0, 0, PACK - 1)
         quantise_h(1, 0, 1)
         features(1, 2)
-        quantise_state_pair(1, 0)
+        quantise_state(1, 0, 1)
         features(1, 3)
         for t in range(PACK):
             flow(0, t)
         quantise_h(1, 2, 3)
-        quantise_state_pair(1, 1)
+        quantise_state(1, 2, 3)
         for t in range(PACK):
             flow(1, t)
             project(t)
-        round_y(0, 1, on_vector)
-        round_y(3, 3, on_scalar)
-        round_y(2, 2, on_vector)
-        planes(0, 1, nc.sync)
-        planes(2, 3, nc.scalar)
+        round_y(on_vector, 0, S // 2)
+        round_y(on_scalar, Y_ON_VECTOR, S)
+        round_y(on_vector, S // 2, Y_ON_VECTOR)
+        planes(0, nc.sync)
+        planes(1, nc.scalar)
         for q in range(QUADS):
             queue = nc.scalar if q % 2 else nc.sync
             queue.dma_start(out=out_2[0, 4 * q : 4 * q + 4, :].bitcast(I32), in_=y_sc[32 * q : 32 * q + 4, :].bitcast(I32))

@@ -29,8 +29,8 @@ QUARTER = P // 4
 Y_ON_VECTOR = 336
 
 SUM_BANKS = 6
-TURN_BANK = 6
-LINE_BANK = (4, 0, 4, 2)
+TURN_BANK = (6, 6, 6, 0)
+LINE_BANK = (4, 6, 4, 2)
 
 
 def tile_list_grid_swing_flow_kernel(
@@ -50,8 +50,6 @@ def tile_list_grid_swing_flow_kernel(
         adj_sc = kept([P, PASSES, H], U8, "adj_sc")
         bus_sc = kept([P, PASSES, H], U8, "bus_sc")
         bus_picked_sc1 = kept([P, S], U8, "bus_picked_sc1")
-        angle0 = kept([P, 1], F32, "angle0")
-        zero = kept([P, 1], F32, "zero")
         ident = kept([P, P], F32, "ident")
         pin = kept([P, PACK], F32, "pin")
         inv = kept([P, PACK], F32, "inv")
@@ -117,7 +115,7 @@ def tile_list_grid_swing_flow_kernel(
         def constants():
             nc.sync.dma_start(out=pin[:], in_=pinj.rearrange("(p t) -> p t", t=PACK))
             nc.sync.dma_start(out=inv[:], in_=minv.rearrange("(p t) -> p t", t=PACK))
-            nc.scalar.activation(out=neg_inv[:], in_=inv[:], func=ACT.Identity, bias=zero[:], scale=-1.0)
+            nc.scalar.activation(out=neg_inv[:], in_=inv[:], func=ACT.Copy, scale=-1.0)
             for t in range(PACK):
                 nc.scalar.activation(out=pin_inv[:, t : t + 1], in_=pin[:, t : t + 1], func=ACT.Copy, scale=inv[:, t : t + 1])
 
@@ -149,7 +147,7 @@ def tile_list_grid_swing_flow_kernel(
             for quarter in range(scalar_quarters):
                 deal(on_scalar, line_bf[c, a], line_raw[c, a], quarter, 1, slice(0, PACK))
             for quarter in range(scalar_quarters, 4, 2):
-                deal(on_vector, line_bf[c, a], line_raw[c, a], quarter, 2, slice(0, PACK))
+                deal(on_vector, line_bf[c, a], line_raw[c, a], quarter, min(2, 4 - quarter), slice(0, PACK))
 
         def quantise(words, plane, values):
             nc.vector.quantize_mx(out=words.bitcast(FP8X4), scales=plane, in_=values)
@@ -197,7 +195,7 @@ def tile_list_grid_swing_flow_kernel(
             nc.vector.tensor_tensor(out=diffs[c, jt][:], in0=by_slot(bus), in1=adj_sb[c, jt][:], op=ALU.subtract)
 
         def sine(c, jt):
-            turned = banks[TURN_BANK + jt % 2]
+            turned = banks[TURN_BANK[2 * c + jt // 2] + jt % 2]
             for t in range(PACK):
                 nc.tensor.transpose(by_group(turned)[:, t, :], diffs[c, jt][:, t, :], ident[:])
             sines[c, jt] = kept([P, P // 2, PACK, 2], F32, "sine%d%d" % (c, jt))
@@ -265,12 +263,10 @@ def tile_list_grid_swing_flow_kernel(
             queue.dma_start(out=words_out[:, js], in_=y_words[:, js].bitcast(I32))
 
         nc.vector.memset(tab_sc[:].bitcast(I32), 0)
-        nc.vector.memset(angle0[:], 0.0)
         nc.vector.memset(adj_sc[:].bitcast(I32), 0)
         nc.vector.memset(bus_sc[:].bitcast(I32), 0)
         nc.vector.memset(bus_picked_sc1[:].bitcast(I32), 0)
         make_identity(nc, ident[:])
-        nc.scalar.activation(out=zero[:], in_=angle0[:], func=ACT.Sin)
 
         load_list("bus", offs)
         load_list("adj", offs2)
@@ -305,30 +301,30 @@ def tile_list_grid_swing_flow_kernel(
         gather_scales("line")
         for a in range(PASSES):
             gather_words("line", a, 0, TILES - 1)
+        round_line(0, 0, 1)
         sines_of(0, 0)
         sums(1, 0)
         sines_of(0, 2)
-        round_line(0, 0, 2)
         quantise_line(0, 0)
         round_line(0, 1, 0)
         quantise_line(0, 1)
         sums(1, 2)
-        round_line(1, 0, 4)
-        round_line(1, 1, 2)
+        round_line(1, 0, 3)
+        round_line(1, 1, 1)
         features(0, 0)
         features(0, 1)
         sines_of(1, 0)
         quantise_line(1, 0)
         quantise_line(1, 1)
+        sines_of(1, 2)
         features(0, 2)
         features(0, 3)
-        sines_of(1, 2)
         for quarter in range(4):
             deal(on_scalar, state_bf[0], state_raw[0], quarter, 1, slice(0, PACK))
-        constants()
-        for copy, slots in ((on_scalar, slice(0, 2)), (on_vector, slice(2, PACK))):
+        for slots in (slice(0, 2), slice(2, PACK)):
             for quarter in (0, 2):
-                deal(copy, state_bf[1], state_raw[1], quarter, 2, slots)
+                deal(on_scalar, state_bf[1], state_raw[1], quarter, 2, slots)
+        constants()
         features(1, 0)
         features(1, 1)
         quantise_h(0, 0, TILES - 1)

@@ -61,6 +61,7 @@ def tile_list_grid_swing_flow_kernel(
         state_bf = [kept([P, PACK, P, PACK], BF16, "state_bf%d" % c) for c in range(PASSES)]
         state_words = [kept([P, N], U32, "state_words%d" % c) for c in range(PASSES)]
         state_sc = [kept([P, N], U8, "state_sc%d" % c) for c in range(PASSES)]
+        warm = kept([P, 2], F32, "warm")
         y = kept([P, PACK, S], F32, "y")
         y_bf = kept([P, S, PACK], BF16, "y_bf")
         y_words = kept([P, S], U32, "y_words")
@@ -74,18 +75,18 @@ def tile_list_grid_swing_flow_kernel(
             lists[name] = keep.tile([P, S // 16], U16, name="list_" + name)
             nc.sync.dma_start(lists[name][:], src)
 
-        def load_table_scales():
+        def load_table_scales(queue):
             for q in range(QUADS):
-                nc.sync.dma_start(
+                queue.dma_start(
                     out=tab_sc[32 * q : 32 * q + 8, :].bitcast(I32),
                     in_=tab_scales[:, 4 * q : 4 * q + 4, :].bitcast(I32),
                 )
 
-        def load_weight_scales(planes, scales):
-            for q in range(QUADS):
-                nc.sync.dma_start(
-                    out=planes[32 * q : 32 * q + 4, :, :].bitcast(I32),
-                    in_=scales[:, 4 * q : 4 * q + 4, :].rearrange("a r c -> r a c").bitcast(I32),
+        def load_weight_scales(queue, planes, scales):
+            for r in range(4):
+                queue.dma_start(
+                    out=planes[r:P:32, :, :].bitcast(I32),
+                    in_=scales[:, r:16:4, :].rearrange("a q c -> q a c").bitcast(I32),
                 )
 
         def load_table(a):
@@ -112,9 +113,11 @@ def tile_list_grid_swing_flow_kernel(
             rows = wstate[PASS * c : PASS * (c + 1), :]
             nc.sync.dma_start(out=state_raw[c][:], in_=rows.rearrange("(p t) n -> p t n", t=PACK))
 
+        def load_constants(queue):
+            queue.dma_start(out=pin[:], in_=pinj.rearrange("(p t) -> p t", t=PACK))
+            queue.dma_start(out=inv[:], in_=minv.rearrange("(p t) -> p t", t=PACK))
+
         def constants():
-            nc.sync.dma_start(out=pin[:], in_=pinj.rearrange("(p t) -> p t", t=PACK))
-            nc.sync.dma_start(out=inv[:], in_=minv.rearrange("(p t) -> p t", t=PACK))
             nc.scalar.activation(out=neg_inv[:], in_=inv[:], func=ACT.Copy, scale=-1.0)
             for t in range(PACK):
                 nc.scalar.activation(out=pin_inv[:, t : t + 1], in_=pin[:, t : t + 1], func=ACT.Copy, scale=inv[:, t : t + 1])
@@ -169,41 +172,45 @@ def tile_list_grid_swing_flow_kernel(
         def by_two(bank):
             return bank[:].rearrange("p (t g e) -> p g t e", t=PACK, e=2)
 
-        def adjacent(c, jt):
+        def adjacent(c, jt, bank, passes=(0, 1)):
             js = slice(P * jt, P * (jt + 1))
-            adj = banks[4 * (2 * c + jt // 2) % SUM_BANKS + jt % 2]
-            for a in range(PASSES):
+            adj = banks[bank]
+            for a in passes:
                 nc.tensor.matmul_mx(
                     out=adj[:], lhsT=picked["adj", a][:, js].bitcast(FP8X4), lhsT_scale=picked_sc["adj"][4 * a :, js],
                     rhs=adj_w[c][:, a, :].bitcast(FP8X4), rhs_scale=adj_sc[:, a, PASS * c : PASS * (c + 1)],
                     start=(a == 0), stop=(a == PASSES - 1),
                 )
+            if passes[-1] == 0:
+                return
             adj_sb[c, jt] = kept([P, PACK, P], F32, "adj_sb%d%d" % (c, jt))
             nc.scalar.copy(out=adj_sb[c, jt][:], in_=by_slot(adj))
 
-        def difference(c, jt):
+        def difference(c, jt, bank, passes=(0, 1)):
             js = slice(P * jt, P * (jt + 1))
-            bus = banks[(4 * (2 * c + jt // 2) + 2) % SUM_BANKS + jt % 2]
-            for a in range(PASSES):
+            bus = banks[bank]
+            for a in passes:
                 nc.tensor.matmul_mx(
                     out=bus[:], lhsT=picked["bus", a][:, js].bitcast(FP8X4),
                     lhsT_scale=(picked_sc["bus"], bus_picked_sc1)[a][:, js],
                     rhs=bus_w[c][:, a, :].bitcast(FP4X4), rhs_scale=bus_sc[:, a, PASS * c : PASS * (c + 1)],
                     start=(a == 0), stop=(a == PASSES - 1),
                 )
+            if passes[-1] == 0:
+                return
             diffs[c, jt] = kept([P, PACK, P], F32, "diff%d%d" % (c, jt))
             nc.vector.tensor_tensor(out=diffs[c, jt][:], in0=by_slot(bus), in1=adj_sb[c, jt][:], op=ALU.subtract)
 
-        def sine(c, jt):
-            turned = banks[TURN_BANK[2 * c + jt // 2] + jt % 2]
+        def sine(c, jt, bank):
+            turned = banks[bank]
             for t in range(PACK):
                 nc.tensor.transpose(by_group(turned)[:, t, :], diffs[c, jt][:, t, :], ident[:])
             sines[c, jt] = kept([P, P // 2, PACK, 2], F32, "sine%d%d" % (c, jt))
             nc.scalar.activation(out=sines[c, jt][:], in_=by_two(turned), func=ACT.Sin)
 
-        def features(c, jt):
+        def features(c, jt, bank):
             js = slice(P * jt, P * (jt + 1))
-            line = banks[LINE_BANK[2 * c + jt // 2] + jt % 2]
+            line = banks[bank]
             for t in range(PACK):
                 ms = slice(P * t, P * (t + 1))
                 for a in (1, 0):
@@ -217,15 +224,25 @@ def tile_list_grid_swing_flow_kernel(
                 out=h_bf[c][:, js, :].rearrange("p (g e) t -> p g t e", e=2), in0=by_two(line), in1=sines[c, jt][:], op=ALU.mult,
             )
 
-        def sums(c, jt):
-            adjacent(c, jt)
-            adjacent(c, jt + 1)
-            difference(c, jt)
-            difference(c, jt + 1)
+        def sums(c, jt, adj_bank, bus_bank):
+            adjacent(c, jt, adj_bank)
+            adjacent(c, jt + 1, adj_bank + 1)
+            difference(c, jt, bus_bank)
+            difference(c, jt + 1, bus_bank + 1)
 
-        def sines_of(c, jt):
-            sine(c, jt)
-            sine(c, jt + 1)
+        def sines_of(c, jt, bank):
+            sine(c, jt, bank)
+            sine(c, jt + 1, bank + 1)
+
+        def features_of(c, jt, bank):
+            features(c, jt, bank)
+            features(c, jt + 1, bank + 1)
+
+        def round_state(c, scalar_quarters):
+            for quarter in range(scalar_quarters):
+                deal(on_scalar, state_bf[c], state_raw[c], quarter, 1, slice(0, PACK))
+            for quarter in range(scalar_quarters, 4, 2):
+                deal(on_vector, state_bf[c], state_raw[c], quarter, min(2, 4 - quarter), slice(0, PACK))
 
         def quantise_h(c, first, last):
             js = slice(P * first, P * (last + 1))
@@ -249,6 +266,35 @@ def tile_list_grid_swing_flow_kernel(
                 )
             nc.sync.dma_start(out=out_0.rearrange("(p t) j -> p t j", t=PACK)[:, t, :], in_=y[:, t, :])
 
+        def flow_part(c, first, last, bank):
+            js = slice(P * first, P * (last + 1))
+            width = js.stop - js.start
+            for t in range(PACK):
+                ms = slice(P * t, P * (t + 1))
+                nc.tensor.matmul_mx(
+                    out=banks[bank + t // 2][:, width * (t % 2) : width * (t % 2 + 1)],
+                    lhsT=state_words[c][:, ms].bitcast(FP8X4), lhsT_scale=state_sc[c][:, ms],
+                    rhs=h_words[c][:, js].bitcast(FP8X4), rhs_scale=h_sc[c][:, js],
+                    start=(c == 0 and t % 2 == 0), stop=(c == PASSES - 1 and t % 2 == 1),
+                )
+
+        def project_part(first, last, bank, pair, on_scalar_engine):
+            js = slice(P * first, P * (last + 1))
+            width = js.stop - js.start
+            for t in (2 * pair, 2 * pair + 1):
+                ts = slice(t, t + 1)
+                src = banks[bank + pair][:, width * (t % 2) : width * (t % 2 + 1)]
+                if on_scalar_engine:
+                    nc.scalar.activation(out=y[:, t, js], in_=src, func=ACT.Identity, bias=pin_inv[:, ts], scale=neg_inv[:, ts])
+                else:
+                    nc.vector.tensor_scalar(
+                        out=y[:, t, js], in0=src, scalar1=neg_inv[:, ts], scalar2=pin_inv[:, ts], op0=ALU.mult, op1=ALU.add,
+                    )
+
+        def store_y(first, last, slots):
+            js = slice(P * first, P * (last + 1))
+            nc.sync.dma_start(out=out_0.rearrange("(p t) j -> p t j", t=PACK)[:, slots, js], in_=y[:, slots, js])
+
         def round_y(copy, first, end):
             gs = slice(first // RUN, end // RUN)
             copy(
@@ -256,37 +302,38 @@ def tile_list_grid_swing_flow_kernel(
                 in_=y[:].rearrange("p t (g e) -> p g t e", e=RUN)[:, gs],
             )
 
-        def planes(half, queue):
-            js = slice(S // 2 * half, S // 2 * (half + 1))
+        def planes(first, last, queue):
+            js = slice(P * first, P * (last + 1))
             quantise(y_words[:, js], y_sc[:, js], y_bf[:, js, :].rearrange("p j t -> p (j t)"))
             words_out = out_1[0].rearrange("p j t -> p (j t)").bitcast(I32)
             queue.dma_start(out=words_out[:, js], in_=y_words[:, js].bitcast(I32))
 
-        nc.vector.memset(tab_sc[:].bitcast(I32), 0)
-        nc.vector.memset(adj_sc[:].bitcast(I32), 0)
+        nc.gpsimd.memset(tab_sc[:].bitcast(I32), 0)
         nc.vector.memset(bus_sc[:].bitcast(I32), 0)
+        nc.vector.memset(adj_sc[:].bitcast(I32), 0)
         nc.vector.memset(bus_picked_sc1[:].bitcast(I32), 0)
-        make_identity(nc, ident[:])
-
-        load_list("bus", offs)
         load_list("adj", offs2)
-        load_table_scales()
+        load_list("bus", offs)
+        load_table_scales(nc.sync)
+        load_weight_scales(nc.gpsimd, bus_sc, wbus_scales)
+        make_identity(nc, ident[:])
+        nc.vector.memset(warm[:, 0:1], 0.0)
+        nc.scalar.activation(out=warm[:, 1:2], in_=warm[:, 0:1], func=ACT.Sin)
         load_table(0)
-        load_table(1)
-        load_weight_scales(adj_sc, wadj_scales)
         load_adj(0)
-        load_list("line", offs3)
-        load_weight_scales(bus_sc, wbus_scales)
+        load_weight_scales(nc.sync, adj_sc, wadj_scales)
         load_bus(0)
-        load_line(0, 0)
+        load_list("line", offs3)
+        load_table(1)
         load_adj(1)
         load_bus(1)
+        load_line(0, 0)
         load_line(0, 1)
         load_line(1, 0)
         load_line(1, 1)
         load_state(0)
         load_state(1)
-
+        load_constants(nc.sync)
         gather_scales("bus")
         shift_bus_plane()
         gather_scales("adj")
@@ -295,56 +342,72 @@ def tile_list_grid_swing_flow_kernel(
         for first in (0, 2):
             gather_words("adj", 1, first, first + 1)
             gather_words("bus", 1, first, first + 1)
-
-        sums(0, 0)
-        sums(0, 2)
         gather_scales("line")
-        for a in range(PASSES):
-            gather_words("line", a, 0, TILES - 1)
-        round_line(0, 0, 1)
-        sines_of(0, 0)
-        sums(1, 0)
-        sines_of(0, 2)
+        gather_words("line", 0, 0, TILES - 1)
+        gather_words("line", 1, 0, TILES - 1)
+        for jt in range(4):
+            adjacent(0, jt, jt, (0,))
+        for jt in range(4):
+            difference(0, jt, 4 + jt, (0,))
+        for first in (0, 2):
+            for jt in (first, first + 1):
+                adjacent(0, jt, jt, (1,))
+            for jt in (first, first + 1):
+                difference(0, jt, 4 + jt, (1,))
+        adjacent(1, 0, 0)
+        adjacent(1, 1, 1)
+        sines_of(0, 0, 2)
+        difference(1, 0, 4)
+        difference(1, 1, 5)
+        round_line(0, 0, 2)
+        sines_of(0, 2, 6)
         quantise_line(0, 0)
-        round_line(0, 1, 0)
+        round_line(0, 1, 1)
         quantise_line(0, 1)
-        sums(1, 2)
-        round_line(1, 0, 3)
+        adjacent(1, 2, 0)
+        adjacent(1, 3, 1)
+        difference(1, 2, 2)
+        difference(1, 3, 3)
+        round_line(1, 0, 2)
+        sines_of(1, 0, 4)
         round_line(1, 1, 1)
-        features(0, 0)
-        features(0, 1)
-        sines_of(1, 0)
         quantise_line(1, 0)
         quantise_line(1, 1)
-        sines_of(1, 2)
-        features(0, 2)
-        features(0, 3)
-        for quarter in range(4):
-            deal(on_scalar, state_bf[0], state_raw[0], quarter, 1, slice(0, PACK))
-        for slots in (slice(0, 2), slice(2, PACK)):
-            for quarter in (0, 2):
-                deal(on_scalar, state_bf[1], state_raw[1], quarter, 2, slots)
+        features_of(0, 0, 6)
+        features_of(0, 2, 0)
+        round_state(0, 4)
         constants()
-        features(1, 0)
-        features(1, 1)
-        quantise_h(0, 0, TILES - 1)
-        quantise_state(0, 0, PACK - 1)
+        features_of(1, 0, 2)
+        quantise_h(0, 0, 3)
+        quantise_state(0, 0, 3)
+        round_state(1, 3)
         quantise_h(1, 0, 1)
-        features(1, 2)
-        quantise_state(1, 0, 1)
-        features(1, 3)
-        for t in range(PACK):
-            flow(0, t)
-        quantise_h(1, 2, 3)
-        quantise_state(1, 2, 3)
-        for t in range(PACK):
-            flow(1, t)
-            project(t)
-        round_y(on_vector, 0, S // 2)
-        round_y(on_scalar, Y_ON_VECTOR, S)
-        round_y(on_vector, S // 2, Y_ON_VECTOR)
-        planes(0, nc.sync)
-        planes(1, nc.scalar)
+        quantise_state(1, 0, 3)
+        sines_of(1, 2, 2)
+        flow_part(0, 0, 1, 6)
+        flow_part(0, 2, 2, 0)
+        flow_part(1, 0, 1, 6)
+        features_of(1, 2, 4)
+        flow_part(0, 3, 3, 2)
+        project_part(0, 1, 6, 0, True)
+        store_y(0, 1, slice(0, 2))
+        project_part(0, 1, 6, 1, True)
+        store_y(0, 1, slice(2, 4))
+        quantise_h(1, 2, 2)
+        flow_part(1, 2, 2, 0)
+        quantise_h(1, 3, 3)
+        flow_part(1, 3, 3, 2)
+        project_part(2, 2, 0, 1, False)
+        project_part(3, 3, 2, 1, False)
+        project_part(2, 2, 0, 0, True)
+        project_part(3, 3, 2, 0, True)
+        store_y(2, 3, slice(0, 2))
+        store_y(2, 3, slice(2, 4))
+        round_y(on_vector, 0, 256)
+        round_y(on_scalar, 256, 384)
+        round_y(on_vector, 384, 512)
+        planes(0, 1, nc.scalar)
+        planes(2, 3, nc.scalar)
         for q in range(QUADS):
             queue = nc.scalar if q % 2 else nc.sync
             queue.dma_start(out=out_2[0, 4 * q : 4 * q + 4, :].bitcast(I32), in_=y_sc[32 * q : 32 * q + 4, :].bitcast(I32))

@@ -28,7 +28,8 @@ SHIFTED_ROWS = 100
 QUARTER = P // 4
 Y_ON_VECTOR = 336
 
-SUM_BANKS = 6
+LATE_SINES = ()
+FREE_TILES = 0
 TURN_BANK = (6, 6, 6, 0)
 LINE_BANK = (4, 6, 4, 2)
 
@@ -55,7 +56,9 @@ def tile_list_grid_swing_flow_kernel(
         inv = kept([P, PACK], F32, "inv")
         neg_inv = kept([P, PACK], F32, "neg_inv")
         pin_inv = kept([P, PACK], F32, "pin_inv")
-        h_bf = [kept([P, S, PACK], BF16, "h_bf%d" % c) for c in range(PASSES)]
+        h_late = kept([P, S, PACK], BF16, "h_late")
+        last_piece = kept([P, FREE_TILES * P * PACK // 2 + PACK * PASS], F32, "last_piece")
+        line_bf1 = kept([P, PASSES, PACK, P, PACK], BF16, "line_bf1")
         h_words = [kept([P, S], U32, "h_words%d" % c) for c in range(PASSES)]
         h_sc = [kept([P, S], U8, "h_sc%d" % c) for c in range(PASSES)]
         state_bf = [kept([P, PACK, P, PACK], BF16, "state_bf%d" % c) for c in range(PASSES)]
@@ -104,7 +107,10 @@ def tile_list_grid_swing_flow_kernel(
             nc.sync.dma_start(out=bus_w[c][:].bitcast(I32), in_=words[:, :, 2 * PASS * c : 2 * PASS * (c + 1)].bitcast(I32))
 
         def load_line(c, a):
-            line_raw[c, a] = kept([P, PACK, PASS], F32, "line_raw%d%d" % (c, a))
+            if (c, a) == (1, 1):
+                line_raw[c, a] = last_piece[:, FREE_TILES * P * PACK // 2 :].rearrange("p (i r) -> p i r", i=PACK)
+            else:
+                line_raw[c, a] = kept([P, PACK, PASS], F32, "line_raw%d%d" % (c, a))
             rows = wline[PASS * a : PASS * (a + 1), PASS * c : PASS * (c + 1)]
             nc.sync.dma_start(out=line_raw[c, a][:], in_=rows.rearrange("(p i) r -> p i r", i=PACK))
 
@@ -146,7 +152,7 @@ def tile_list_grid_swing_flow_kernel(
             )
 
         def round_line(c, a, scalar_quarters):
-            line_bf[c, a] = kept([P, PACK, P, PACK], BF16, "line_bf%d%d" % (c, a))
+            line_bf[c, a] = line_bf1[:, a] if c else kept([P, PACK, P, PACK], BF16, "line_bf%d%d" % (c, a))
             for quarter in range(scalar_quarters):
                 deal(on_scalar, line_bf[c, a], line_raw[c, a], quarter, 1, slice(0, PACK))
             for quarter in range(scalar_quarters, 4, 2):
@@ -158,6 +164,12 @@ def tile_list_grid_swing_flow_kernel(
         def quantise_line(c, a):
             line_q[c, a] = (kept([P, PASS], U32, "line_words%d%d" % (c, a)), kept([P, PASS], U8, "line_sc%d%d" % (c, a)))
             quantise(line_q[c, a][0][:], line_q[c, a][1][:], line_bf[c, a][:].rearrange("p t m i -> p (t m i)"))
+
+        def quantise_lines(c):
+            words, plane = kept([P, PASSES, PASS], U32, "line_words1"), kept([P, PASSES, PASS], U8, "line_sc1")
+            quantise(words[:].rearrange("p a m -> p (a m)"), plane[:].rearrange("p a m -> p (a m)"), line_bf1[:].rearrange("p a t m i -> p (a t m i)"))
+            for a in range(PASSES):
+                line_q[c, a] = (words[:, a, :], plane[:, a, :])
 
         def quantise_state(c, first, last):
             ms = slice(P * first, P * (last + 1))
@@ -205,8 +217,17 @@ def tile_list_grid_swing_flow_kernel(
             turned = banks[bank]
             for t in range(PACK):
                 nc.tensor.transpose(by_group(turned)[:, t, :], diffs[c, jt][:, t, :], ident[:])
-            sines[c, jt] = kept([P, P // 2, PACK, 2], F32, "sine%d%d" % (c, jt))
-            nc.scalar.activation(out=sines[c, jt][:], in_=by_two(turned), func=ACT.Sin)
+            if (c, jt) in LATE_SINES:
+                sines[c, jt] = state_raw[1][:, jt, :].rearrange("p (g t e) -> p g t e", t=PACK, e=2)
+            else:
+                sines[c, jt] = kept([P, P // 2, PACK, 2], F32, "sine%d%d" % (c, jt))[:]
+            nc.scalar.activation(out=sines[c, jt], in_=by_two(turned), func=ACT.Sin)
+
+        def h_rounded(c, first, last):
+            if c == 1 and first >= 2:
+                return state_raw[1][:, first, N // 2 :].bitcast(BF16).rearrange("p (j t) -> p j t", t=PACK)
+            home = h_late[:] if c else last_piece[:, : S * PACK // 2].bitcast(BF16).rearrange("p (j t) -> p j t", t=PACK)
+            return home[:, P * first : P * (last + 1), :]
 
         def features(c, jt, bank):
             js = slice(P * jt, P * (jt + 1))
@@ -221,7 +242,7 @@ def tile_list_grid_swing_flow_kernel(
                         start=(a == 1), stop=(a == 0),
                     )
             nc.vector.tensor_tensor(
-                out=h_bf[c][:, js, :].rearrange("p (g e) t -> p g t e", e=2), in0=by_two(line), in1=sines[c, jt][:], op=ALU.mult,
+                out=h_rounded(c, jt, jt).rearrange("p (g e) t -> p g t e", e=2), in0=by_two(line), in1=sines[c, jt], op=ALU.mult,
             )
 
         def sums(c, jt, adj_bank, bus_bank):
@@ -246,7 +267,7 @@ def tile_list_grid_swing_flow_kernel(
 
         def quantise_h(c, first, last):
             js = slice(P * first, P * (last + 1))
-            quantise(h_words[c][:, js], h_sc[c][:, js], h_bf[c][:, js, :].rearrange("p j t -> p (j t)"))
+            quantise(h_words[c][:, js], h_sc[c][:, js], h_rounded(c, first, last).rearrange("p j t -> p (j t)"))
 
         def flow(c, t):
             ms = slice(P * t, P * (t + 1))
@@ -315,19 +336,19 @@ def tile_list_grid_swing_flow_kernel(
         load_list("adj", offs2)
         load_list("bus", offs)
         load_table_scales(nc.sync)
-        load_weight_scales(nc.gpsimd, bus_sc, wbus_scales)
         make_identity(nc, ident[:])
         nc.vector.memset(warm[:, 0:1], 0.0)
         nc.scalar.activation(out=warm[:, 1:2], in_=warm[:, 0:1], func=ACT.Sin)
         load_table(0)
         load_adj(0)
         load_weight_scales(nc.sync, adj_sc, wadj_scales)
-        load_bus(0)
         load_list("line", offs3)
         load_table(1)
+        load_weight_scales(nc.sync, bus_sc, wbus_scales)
+        load_bus(0)
+        load_line(0, 0)
         load_adj(1)
         load_bus(1)
-        load_line(0, 0)
         load_line(0, 1)
         load_line(1, 0)
         load_line(1, 1)
@@ -339,73 +360,70 @@ def tile_list_grid_swing_flow_kernel(
         gather_scales("adj")
         gather_words("adj", 0, 0, TILES - 1)
         gather_words("bus", 0, 0, TILES - 1)
-        for first in (0, 2):
-            gather_words("adj", 1, first, first + 1)
-            gather_words("bus", 1, first, first + 1)
+        gather_words("adj", 1, 0, 1)
+        gather_words("adj", 1, 2, 3)
+        gather_words("bus", 1, 0, 1)
+        gather_words("bus", 1, 2, 3)
         gather_scales("line")
         gather_words("line", 0, 0, TILES - 1)
         gather_words("line", 1, 0, TILES - 1)
         for jt in range(4):
             adjacent(0, jt, jt, (0,))
         for jt in range(4):
-            difference(0, jt, 4 + jt, (0,))
-        for first in (0, 2):
-            for jt in (first, first + 1):
-                adjacent(0, jt, jt, (1,))
-            for jt in (first, first + 1):
-                difference(0, jt, 4 + jt, (1,))
+            adjacent(0, jt, jt, (1,))
+        for jt in range(4):
+            difference(0, jt, 4 + jt)
         adjacent(1, 0, 0)
         adjacent(1, 1, 1)
         sines_of(0, 0, 2)
         difference(1, 0, 4)
         difference(1, 1, 5)
-        round_line(0, 0, 2)
-        sines_of(0, 2, 6)
+        round_line(0, 0, 1)
+        sines_of(0, 2, 0)
         quantise_line(0, 0)
-        round_line(0, 1, 1)
+        round_line(0, 1, 0)
         quantise_line(0, 1)
-        adjacent(1, 2, 0)
-        adjacent(1, 3, 1)
+        adjacent(1, 2, 6)
+        adjacent(1, 3, 7)
         difference(1, 2, 2)
         difference(1, 3, 3)
-        round_line(1, 0, 2)
+        round_line(1, 0, 3)
         sines_of(1, 0, 4)
-        round_line(1, 1, 1)
-        quantise_line(1, 0)
-        quantise_line(1, 1)
+        round_line(1, 1, 0)
+        quantise_lines(1)
         features_of(0, 0, 6)
-        features_of(0, 2, 0)
+        sines_of(1, 2, 0)
+        features_of(0, 2, 4)
         round_state(0, 4)
-        constants()
-        features_of(1, 0, 2)
         quantise_h(0, 0, 3)
         quantise_state(0, 0, 3)
+        features_of(1, 0, 2)
         round_state(1, 3)
+        constants()
         quantise_h(1, 0, 1)
         quantise_state(1, 0, 3)
-        sines_of(1, 2, 2)
-        flow_part(0, 0, 1, 6)
-        flow_part(0, 2, 2, 0)
-        flow_part(1, 0, 1, 6)
-        features_of(1, 2, 4)
-        flow_part(0, 3, 3, 2)
-        project_part(0, 1, 6, 0, True)
+        flow_part(0, 0, 1, 4)
+        flow_part(0, 2, 2, 6)
+        flow_part(1, 0, 1, 4)
+        features_of(1, 2, 2)
+        flow_part(0, 3, 3, 0)
+        project_part(0, 1, 4, 0, True)
         store_y(0, 1, slice(0, 2))
-        project_part(0, 1, 6, 1, True)
+        project_part(0, 1, 4, 1, True)
         store_y(0, 1, slice(2, 4))
         quantise_h(1, 2, 2)
-        flow_part(1, 2, 2, 0)
+        flow_part(1, 2, 2, 6)
         quantise_h(1, 3, 3)
-        flow_part(1, 3, 3, 2)
-        project_part(2, 2, 0, 1, False)
-        project_part(3, 3, 2, 1, False)
-        project_part(2, 2, 0, 0, True)
-        project_part(3, 3, 2, 0, True)
-        store_y(2, 3, slice(0, 2))
-        store_y(2, 3, slice(2, 4))
-        round_y(on_vector, 0, 256)
-        round_y(on_scalar, 256, 384)
-        round_y(on_vector, 384, 512)
+        flow_part(1, 3, 3, 0)
+        project_part(2, 2, 6, 1, False)
+        project_part(3, 3, 0, 1, False)
+        project_part(2, 2, 6, 0, True)
+        project_part(3, 3, 0, 0, True)
+        store_y(2, 3, slice(0, 4))
+        round_y(on_scalar, 0, 128)
+        round_y(on_vector, 128, 256)
+        round_y(on_vector, 256, 432)
+        round_y(on_scalar, 432, 512)
         planes(0, 1, nc.scalar)
         planes(2, 3, nc.scalar)
         for q in range(QUADS):

@@ -50,7 +50,10 @@ def tile_list_grid_swing_flow_kernel(
         tab_sc = kept([P, T], U8, "tab_sc")
         adj_sc = kept([P, PASSES, H], U8, "adj_sc")
         bus_sc = kept([P, PASSES, H], U8, "bus_sc")
-        bus_picked_sc1 = kept([P, S], U8, "bus_picked_sc1")
+        sums_sc = kept([P, 2 * S], U8, "sums_sc")
+        sums_sc1 = kept([P, 2 * S], U8, "sums_sc1")
+        line_sc1 = kept([P, S], U8, "line_sc1_picked")
+        shifted = {"bus": sums_sc1[:, 0:S], "adj": sums_sc1[:, S : 2 * S], "line": line_sc1[:]}
         ident = kept([P, P], F32, "ident")
         pin = kept([P, PACK], F32, "pin")
         inv = kept([P, PACK], F32, "inv")
@@ -79,10 +82,10 @@ def tile_list_grid_swing_flow_kernel(
             nc.sync.dma_start(lists[name][:], src)
 
         def load_table_scales(queue):
-            for q in range(QUADS):
+            for r in range(4):
                 queue.dma_start(
-                    out=tab_sc[32 * q : 32 * q + 8, :].bitcast(I32),
-                    in_=tab_scales[:, 4 * q : 4 * q + 4, :].bitcast(I32),
+                    out=tab_sc[r:P:16, :].bitcast(I32),
+                    in_=tab_scales[:, r:16:4, :].rearrange("a q t -> q a t").bitcast(I32),
                 )
 
         def load_weight_scales(queue, planes, scales):
@@ -129,8 +132,11 @@ def tile_list_grid_swing_flow_kernel(
                 nc.scalar.activation(out=pin_inv[:, t : t + 1], in_=pin[:, t : t + 1], func=ACT.Copy, scale=inv[:, t : t + 1])
 
         def gather_scales(name):
-            picked_sc[name] = kept([P, S], U8, "picked_sc_" + name)
-            nc.vector.tensor_copy(picked_sc[name][:], tab_sc[:].indirect(lists[name][:]))
+            if name == "line":
+                picked_sc[name] = kept([P, S], U8, "picked_sc_line")[:]
+            else:
+                picked_sc[name] = sums_sc[:, 0:S] if name == "bus" else sums_sc[:, S : 2 * S]
+            nc.vector.tensor_copy(picked_sc[name], tab_sc[:].indirect(lists[name][:]))
 
         def gather_words(name, a, first, last):
             if first == 0:
@@ -138,11 +144,8 @@ def tile_list_grid_swing_flow_kernel(
             offsets = lists[name][:, P // 16 * first : P // 16 * (last + 1)]
             nc.vector.tensor_copy(picked[name, a][:, P * first : P * (last + 1)], tab_w[a][:].indirect(offsets))
 
-        def shift_bus_plane():
-            nc.scalar.dma_start(
-                out=bus_picked_sc1[0:SHIFTED_ROWS, :].bitcast(I32),
-                in_=picked_sc["bus"][4 : 4 + SHIFTED_ROWS, :].bitcast(I32),
-            )
+        def shift_plane(home, source):
+            nc.scalar.dma_start(out=home[0:SHIFTED_ROWS, :].bitcast(I32), in_=source[16 : 16 + SHIFTED_ROWS, :].bitcast(I32))
 
         def deal(copy, rounded, raw, quarter, quarters, slots):
             ms = slice(QUARTER * quarter, QUARTER * (quarter + quarters))
@@ -189,7 +192,7 @@ def tile_list_grid_swing_flow_kernel(
             adj = banks[bank]
             for a in passes:
                 nc.tensor.matmul_mx(
-                    out=adj[:], lhsT=picked["adj", a][:, js].bitcast(FP8X4), lhsT_scale=picked_sc["adj"][4 * a :, js],
+                    out=adj[:], lhsT=picked["adj", a][:, js].bitcast(FP8X4), lhsT_scale=(picked_sc, shifted)[a]["adj"][:, js],
                     rhs=adj_w[c][:, a, :].bitcast(FP8X4), rhs_scale=adj_sc[:, a, PASS * c : PASS * (c + 1)],
                     start=(a == 0), stop=(a == PASSES - 1),
                 )
@@ -204,7 +207,7 @@ def tile_list_grid_swing_flow_kernel(
             for a in passes:
                 nc.tensor.matmul_mx(
                     out=bus[:], lhsT=picked["bus", a][:, js].bitcast(FP8X4),
-                    lhsT_scale=(picked_sc["bus"], bus_picked_sc1)[a][:, js],
+                    lhsT_scale=(picked_sc, shifted)[a]["bus"][:, js],
                     rhs=bus_w[c][:, a, :].bitcast(FP4X4), rhs_scale=bus_sc[:, a, PASS * c : PASS * (c + 1)],
                     start=(a == 0), stop=(a == PASSES - 1),
                 )
@@ -238,7 +241,7 @@ def tile_list_grid_swing_flow_kernel(
                     words, plane = line_q[c, a]
                     nc.tensor.matmul_mx(
                         out=by_group(line)[:, t, :], lhsT=words[:, ms].bitcast(FP8X4), lhsT_scale=plane[:, ms],
-                        rhs=picked["line", a][:, js].bitcast(FP8X4), rhs_scale=picked_sc["line"][4 * a :, js],
+                        rhs=picked["line", a][:, js].bitcast(FP8X4), rhs_scale=(picked_sc, shifted)[a]["line"][:, js],
                         start=(a == 1), stop=(a == 0),
                     )
             nc.vector.tensor_tensor(
@@ -332,7 +335,8 @@ def tile_list_grid_swing_flow_kernel(
         nc.gpsimd.memset(tab_sc[:].bitcast(I32), 0)
         nc.vector.memset(bus_sc[:].bitcast(I32), 0)
         nc.vector.memset(adj_sc[:].bitcast(I32), 0)
-        nc.vector.memset(bus_picked_sc1[:].bitcast(I32), 0)
+        nc.vector.memset(sums_sc1[:].bitcast(I32), 0)
+        nc.vector.memset(line_sc1[:].bitcast(I32), 0)
         load_list("adj", offs2)
         load_list("bus", offs)
         load_table_scales(nc.sync)
@@ -356,8 +360,8 @@ def tile_list_grid_swing_flow_kernel(
         load_state(1)
         load_constants(nc.sync)
         gather_scales("bus")
-        shift_bus_plane()
         gather_scales("adj")
+        shift_plane(sums_sc1, sums_sc)
         gather_words("adj", 0, 0, TILES - 1)
         gather_words("bus", 0, 0, TILES - 1)
         gather_words("adj", 1, 0, 1)
@@ -365,6 +369,7 @@ def tile_list_grid_swing_flow_kernel(
         gather_words("bus", 1, 0, 1)
         gather_words("bus", 1, 2, 3)
         gather_scales("line")
+        shift_plane(line_sc1, picked_sc["line"])
         gather_words("line", 0, 0, TILES - 1)
         gather_words("line", 1, 0, TILES - 1)
         for jt in range(4):

@@ -144,8 +144,8 @@ def tile_list_grid_swing_flow_kernel(
             offsets = lists[name][:, P // 16 * first : P // 16 * (last + 1)]
             nc.vector.tensor_copy(picked[name, a][:, P * first : P * (last + 1)], tab_w[a][:].indirect(offsets))
 
-        def shift_plane(home, source):
-            nc.scalar.dma_start(out=home[0:SHIFTED_ROWS, :].bitcast(I32), in_=source[16 : 16 + SHIFTED_ROWS, :].bitcast(I32))
+        def shift_plane(queue, home, source):
+            queue.dma_start(out=home[0:SHIFTED_ROWS, :].bitcast(I32), in_=source[16 : 16 + SHIFTED_ROWS, :].bitcast(I32))
 
         def deal(copy, rounded, raw, quarter, quarters, slots):
             ms = slice(QUARTER * quarter, QUARTER * (quarter + quarters))
@@ -348,28 +348,28 @@ def tile_list_grid_swing_flow_kernel(
         load_weight_scales(nc.sync, adj_sc, wadj_scales)
         load_list("line", offs3)
         load_table(1)
+        gather_scales("bus")
+        gather_scales("adj")
+        shift_plane(nc.sync, sums_sc1, sums_sc)
         load_weight_scales(nc.sync, bus_sc, wbus_scales)
         load_bus(0)
         load_line(0, 0)
         load_adj(1)
         load_bus(1)
+        gather_scales("line")
+        shift_plane(nc.sync, line_sc1, picked_sc["line"])
         load_line(0, 1)
         load_line(1, 0)
         load_line(1, 1)
         load_state(0)
         load_state(1)
         load_constants(nc.sync)
-        gather_scales("bus")
-        gather_scales("adj")
-        shift_plane(sums_sc1, sums_sc)
         gather_words("adj", 0, 0, TILES - 1)
         gather_words("bus", 0, 0, TILES - 1)
         gather_words("adj", 1, 0, 1)
         gather_words("adj", 1, 2, 3)
         gather_words("bus", 1, 0, 1)
         gather_words("bus", 1, 2, 3)
-        gather_scales("line")
-        shift_plane(line_sc1, picked_sc["line"])
         gather_words("line", 0, 0, TILES - 1)
         gather_words("line", 1, 0, TILES - 1)
         for jt in range(4):

@@ -44,8 +44,8 @@ def tile_list_grid_swing_flow_kernel(
         psum = ctx.enter_context(tc.psum_pool(name="psum", bufs=1))
         banks = [psum.tile([P, PASS], F32, name="bank%d" % b) for b in range(8)]
 
-        def kept(shape, dtype, name):
-            return keep.tile(shape, dtype, name=name, align_bytes=64)
+        def kept(shape, dtype, name, tag=None):
+            return keep.tile(shape, dtype, name=name, tag=tag or name, align_bytes=64)
 
         tab_sc = kept([P, T], U8, "tab_sc")
         adj_sc = kept([P, PASSES, H], U8, "adj_sc")
@@ -140,7 +140,7 @@ def tile_list_grid_swing_flow_kernel(
 
         def gather_words(name, a, first, last):
             if first == 0:
-                picked[name, a] = kept([P, S], U32, "picked_%s%d" % (name, a))
+                picked[name, a] = kept([P, S], U32, "picked_%s%d" % (name, a), "adj_sb0%d" % (2 + a) if name == "line" else None)
             offsets = lists[name][:, P // 16 * first : P // 16 * (last + 1)]
             nc.vector.tensor_copy(picked[name, a][:, P * first : P * (last + 1)], tab_w[a][:].indirect(offsets))
 
@@ -353,9 +353,9 @@ def tile_list_grid_swing_flow_kernel(
         shift_plane(nc.sync, sums_sc1, sums_sc)
         load_weight_scales(nc.sync, bus_sc, wbus_scales)
         load_bus(0)
-        load_line(0, 0)
         load_adj(1)
         load_bus(1)
+        load_line(0, 0)
         gather_scales("line")
         shift_plane(nc.sync, line_sc1, picked_sc["line"])
         load_line(0, 1)
@@ -370,20 +370,20 @@ def tile_list_grid_swing_flow_kernel(
         gather_words("adj", 1, 2, 3)
         gather_words("bus", 1, 0, 1)
         gather_words("bus", 1, 2, 3)
-        gather_words("line", 0, 0, TILES - 1)
-        gather_words("line", 1, 0, TILES - 1)
         for jt in range(4):
             adjacent(0, jt, jt, (0,))
         for jt in range(4):
             adjacent(0, jt, jt, (1,))
         for jt in range(4):
             difference(0, jt, 4 + jt)
+        gather_words("line", 0, 0, TILES - 1)
+        gather_words("line", 1, 0, TILES - 1)
         adjacent(1, 0, 0)
         adjacent(1, 1, 1)
         sines_of(0, 0, 2)
         difference(1, 0, 4)
         difference(1, 1, 5)
-        round_line(0, 0, 1)
+        round_line(0, 0, 2)
         sines_of(0, 2, 0)
         quantise_line(0, 0)
         round_line(0, 1, 0)
@@ -392,7 +392,7 @@ def tile_list_grid_swing_flow_kernel(
         adjacent(1, 3, 7)
         difference(1, 2, 2)
         difference(1, 3, 3)
-        round_line(1, 0, 3)
+        round_line(1, 0, 4)
         sines_of(1, 0, 4)
         round_line(1, 1, 0)
         quantise_lines(1)

@@ -140,7 +140,7 @@ def tile_list_grid_swing_flow_kernel(
 
         def gather_words(name, a, first, last):
             if first == 0:
-                picked[name, a] = kept([P, S], U32, "picked_%s%d" % (name, a), "adj_sb0%d" % (2 + a) if name == "line" else None)
+                picked[name, a] = kept([P, S], U32, "picked_%s%d" % (name, a), ("adj_w0", "adj_sb03")[a] if name == "line" else None)
             offsets = lists[name][:, P // 16 * first : P // 16 * (last + 1)]
             nc.vector.tensor_copy(picked[name, a][:, P * first : P * (last + 1)], tab_w[a][:].indirect(offsets))
 
@@ -374,9 +374,9 @@ def tile_list_grid_swing_flow_kernel(
             adjacent(0, jt, jt, (0,))
         for jt in range(4):
             adjacent(0, jt, jt, (1,))
+        gather_words("line", 0, 0, TILES - 1)
         for jt in range(4):
             difference(0, jt, 4 + jt)
-        gather_words("line", 0, 0, TILES - 1)
         gather_words("line", 1, 0, TILES - 1)
         adjacent(1, 0, 0)
         adjacent(1, 1, 1)

@@ -232,18 +232,27 @@ def tile_list_grid_swing_flow_kernel(
             home = h_late[:] if c else last_piece[:, : S * PACK // 2].bitcast(BF16).rearrange("p (j t) -> p j t", t=PACK)
             return home[:, P * first : P * (last + 1), :]
 
-        def features(c, jt, bank):
-            js = slice(P * jt, P * (jt + 1))
+        def line_pass(c, jt, bank, t, a, start, stop):
+            js, ms = slice(P * jt, P * (jt + 1)), slice(P * t, P * (t + 1))
+            words, plane = line_q[c, a]
+            nc.tensor.matmul_mx(
+                out=by_group(banks[bank])[:, t, :], lhsT=words[:, ms].bitcast(FP8X4), lhsT_scale=plane[:, ms],
+                rhs=picked["line", a][:, js].bitcast(FP8X4), rhs_scale=(picked_sc, shifted)[a]["line"][:, js],
+                start=start, stop=stop,
+            )
+
+        def open_line(c, jt, bank):
+            for t in range(PACK):
+                line_pass(c, jt, bank, t, 0, t == 0, False)
+
+        def features(c, jt, bank, opened=False):
             line = banks[bank]
             for t in range(PACK):
-                ms = slice(P * t, P * (t + 1))
-                for a in (1, 0):
-                    words, plane = line_q[c, a]
-                    nc.tensor.matmul_mx(
-                        out=by_group(line)[:, t, :], lhsT=words[:, ms].bitcast(FP8X4), lhsT_scale=plane[:, ms],
-                        rhs=picked["line", a][:, js].bitcast(FP8X4), rhs_scale=(picked_sc, shifted)[a]["line"][:, js],
-                        start=(a == 1), stop=(a == 0),
-                    )
+                if opened:
+                    line_pass(c, jt, bank, t, 1, False, t == PACK - 1)
+                else:
+                    for a in (1, 0):
+                        line_pass(c, jt, bank, t, a, a == 1, a == 0)
             nc.vector.tensor_tensor(
                 out=h_rounded(c, jt, jt).rearrange("p (g e) t -> p g t e", e=2), in0=by_two(line), in1=sines[c, jt], op=ALU.mult,
             )
@@ -394,27 +403,31 @@ def tile_list_grid_swing_flow_kernel(
         difference(1, 3, 3)
         round_line(1, 0, 4)
         sines_of(1, 0, 4)
+        open_line(0, 0, 6)
+        open_line(0, 1, 7)
         round_line(1, 1, 0)
         quantise_lines(1)
-        features_of(0, 0, 6)
+        features(0, 0, 6, True)
+        features(0, 1, 7, True)
         sines_of(1, 2, 0)
-        features_of(0, 2, 4)
+        features(0, 2, 2)
+        features(0, 3, 6)
         round_state(0, 4)
         quantise_h(0, 0, 3)
         quantise_state(0, 0, 3)
-        features_of(1, 0, 2)
+        features_of(1, 0, 4)
         round_state(1, 3)
         constants()
         quantise_h(1, 0, 1)
         quantise_state(1, 0, 3)
-        flow_part(0, 0, 1, 4)
+        flow_part(0, 0, 1, 2)
         flow_part(0, 2, 2, 6)
-        flow_part(1, 0, 1, 4)
-        features_of(1, 2, 2)
+        flow_part(1, 0, 1, 2)
+        features_of(1, 2, 4)
         flow_part(0, 3, 3, 0)
-        project_part(0, 1, 4, 0, True)
+        project_part(0, 1, 2, 0, True)
         store_y(0, 1, slice(0, 2))
-        project_part(0, 1, 4, 1, True)
+        project_part(0, 1, 2, 1, True)
         store_y(0, 1, slice(2, 4))
         quantise_h(1, 2, 2)
         flow_part(1, 2, 2, 6)

from contextlib import ExitStack

import concourse.mybir as mybir
from concourse.masks import make_identity

K, T, S, H, N = 1024, 2048, 512, 1024, 512
FLOPS = 2 * (3 * K * H * S + H * N * S)

F32 = mybir.dt.float32
BF16 = mybir.dt.bfloat16
I32 = mybir.dt.int32
U32 = mybir.dt.uint32
U16 = mybir.dt.uint16
U8 = mybir.dt.uint8
FP8X4 = mybir.dt.float8_e4m3fn_x4
FP4X4 = mybir.dt.float4_e2m1fn_x4
ACT = mybir.ActivationFunctionType
ALU = mybir.AluOpType

P = 128
PACK = 4
PASS = P * PACK
PASSES = 2
QUADS = 4
TILES = S // P
RUN = 4
SHIFTED_ROWS = 100
QUARTER = P // 4
Y_ON_VECTOR = 336

LATE_SINES = ()
FREE_TILES = 0
TURN_BANK = (6, 6, 6, 0)
LINE_BANK = (4, 6, 4, 2)


def tile_list_grid_swing_flow_kernel(
    tc, tab_words, tab_scales, wbus_words, wbus_scales, wadj_words, wadj_scales,
    wline, wstate, pinj, minv, offs, offs2, offs3, out_0, out_1, out_2,
):
    nc = tc.nc
    with ExitStack() as ctx:
        keep = ctx.enter_context(tc.tile_pool(name="keep", bufs=1))
        psum = ctx.enter_context(tc.psum_pool(name="psum", bufs=1))
        banks = [psum.tile([P, PASS], F32, name="bank%d" % b) for b in range(8)]

        def kept(shape, dtype, name, tag=None):
            return keep.tile(shape, dtype, name=name, tag=tag or name, align_bytes=64)

        tab_sc = kept([P, T], U8, "tab_sc")
        adj_sc = kept([P, PASSES, H], U8, "adj_sc")
        bus_sc = kept([P, PASSES, H], U8, "bus_sc")
        sums_sc = kept([P, 2 * S], U8, "sums_sc")
        sums_sc1 = kept([P, 2 * S], U8, "sums_sc1")
        line_sc1 = kept([P, S], U8, "line_sc1_picked")
        shifted = {"bus": sums_sc1[:, 0:S], "adj": sums_sc1[:, S : 2 * S], "line": line_sc1[:]}
        ident = kept([P, P], F32, "ident")
        pin = kept([P, PACK], F32, "pin")
        inv = kept([P, PACK], F32, "inv")
        neg_inv = kept([P, PACK], F32, "neg_inv")
        pin_inv = kept([P, PACK], F32, "pin_inv")
        h_late = kept([P, S, PACK], BF16, "h_late")
        last_piece = kept([P, FREE_TILES * P * PACK // 2 + PACK * PASS], F32, "last_piece")
        line_bf1 = kept([P, PASSES, PACK, P, PACK], BF16, "line_bf1")
        h_words = [kept([P, S], U32, "h_words%d" % c) for c in range(PASSES)]
        h_sc = [kept([P, S], U8, "h_sc%d" % c) for c in range(PASSES)]
        state_bf = [kept([P, PACK, P, PACK], BF16, "state_bf%d" % c) for c in range(PASSES)]
        state_words = [kept([P, N], U32, "state_words%d" % c) for c in range(PASSES)]
        state_sc = [kept([P, N], U8, "state_sc%d" % c) for c in range(PASSES)]
        warm = kept([P, 2], F32, "warm")
        y = kept([P, PACK, S], F32, "y")
        y_bf = kept([P, S, PACK], BF16, "y_bf")
        y_words = kept([P, S], U32, "y_words")
        y_sc = kept([P, S], U8, "y_sc")
        lists, tab_w, adj_w, bus_w, line_raw, state_raw = {}, {}, {}, {}, {}, {}
        picked, picked_sc, line_bf, line_q = {}, {}, {}, {}
        adj_sb, diffs, sines = {}, {}, {}
        on_scalar, on_vector = nc.scalar.copy, nc.vector.tensor_copy

        def load_list(name, src):
            lists[name] = keep.tile([P, S // 16], U16, name="list_" + name)
            nc.sync.dma_start(lists[name][:], src)

        def load_table_scales(queue):
            for r in range(4):
                queue.dma_start(
                    out=tab_sc[r:P:16, :].bitcast(I32),
                    in_=tab_scales[:, r:16:4, :].rearrange("a q t -> q a t").bitcast(I32),
                )

        def load_weight_scales(queue, planes, scales):
            for r in range(4):
                queue.dma_start(
                    out=planes[r:P:32, :, :].bitcast(I32),
                    in_=scales[:, r:16:4, :].rearrange("a q c -> q a c").bitcast(I32),
                )

        def load_table(a):
            tab_w[a] = kept([P, T], U32, "tab_w%d" % a)
            nc.sync.dma_start(out=tab_w[a][:].bitcast(I32), in_=tab_words[a].rearrange("p t i -> p (t i)").bitcast(I32))

        def load_adj(c):
            adj_w[c] = kept([P, PASSES, PASS], U32, "adj_w%d" % c)
            words = wadj_words.rearrange("a p c i -> p a (c i)")
            nc.sync.dma_start(out=adj_w[c][:].bitcast(I32), in_=words[:, :, 4 * PASS * c : 4 * PASS * (c + 1)].bitcast(I32))

        def load_bus(c):
            bus_w[c] = kept([P, PASSES, 2 * PASS], U8, "bus_w%d" % c)
            words = wbus_words.rearrange("a p c -> p a c")
            nc.sync.dma_start(out=bus_w[c][:].bitcast(I32), in_=words[:, :, 2 * PASS * c : 2 * PASS * (c + 1)].bitcast(I32))

        def load_line(c, a):
            if (c, a) == (1, 1):
                line_raw[c, a] = last_piece[:, FREE_TILES * P * PACK // 2 :].rearrange("p (i r) -> p i r", i=PACK)
            else:
                line_raw[c, a] = kept([P, PACK, PASS], F32, "line_raw%d%d" % (c, a))
            rows = wline[PASS * a : PASS * (a + 1), PASS * c : PASS * (c + 1)]
            nc.sync.dma_start(out=line_raw[c, a][:], in_=rows.rearrange("(p i) r -> p i r", i=PACK))

        def load_state(c):
            state_raw[c] = kept([P, PACK, N], F32, "state_raw%d" % c)
            rows = wstate[PASS * c : PASS * (c + 1), :]
            nc.sync.dma_start(out=state_raw[c][:], in_=rows.rearrange("(p t) n -> p t n", t=PACK))

        def load_constants(queue):
            queue.dma_start(out=pin[:], in_=pinj.rearrange("(p t) -> p t", t=PACK))
            queue.dma_start(out=inv[:], in_=minv.rearrange("(p t) -> p t", t=PACK))

        def constants():
            nc.scalar.activation(out=neg_inv[:], in_=inv[:], func=ACT.Copy, scale=-1.0)
            for t in range(PACK):
                nc.scalar.activation(out=pin_inv[:, t : t + 1], in_=pin[:, t : t + 1], func=ACT.Copy, scale=inv[:, t : t + 1])

        def gather_scales(name):
            if name == "line":
                picked_sc[name] = kept([P, S], U8, "picked_sc_line")[:]
            else:
                picked_sc[name] = sums_sc[:, 0:S] if name == "bus" else sums_sc[:, S : 2 * S]
            nc.vector.tensor_copy(picked_sc[name], tab_sc[:].indirect(lists[name][:]))

        def gather_words(name, a, first, last):
            if first == 0:
                picked[name, a] = kept([P, S], U32, "picked_%s%d" % (name, a), ("adj_w0", "adj_sb03")[a] if name == "line" else None)
            offsets = lists[name][:, P // 16 * first : P // 16 * (last + 1)]
            nc.vector.tensor_copy(picked[name, a][:, P * first : P * (last + 1)], tab_w[a][:].indirect(offsets))

        def shift_plane(queue, home, source):
            queue.dma_start(out=home[0:SHIFTED_ROWS, :].bitcast(I32), in_=source[16 : 16 + SHIFTED_ROWS, :].bitcast(I32))

        def deal(copy, rounded, raw, quarter, quarters, slots):
            ms = slice(QUARTER * quarter, QUARTER * (quarter + quarters))
            copy(
                out=rounded[:].rearrange("p t m i -> p m i t")[:, ms, :, slots],
                in_=raw[:].rearrange("p i (m t) -> p m i t", t=PACK)[:, ms, :, slots],
            )

        def round_line(c, a, scalar_quarters):
            line_bf[c, a] = line_bf1[:, a] if c else kept([P, PACK, P, PACK], BF16, "line_bf%d%d" % (c, a))
            for quarter in range(scalar_quarters):
                deal(on_scalar, line_bf[c, a], line_raw[c, a], quarter, 1, slice(0, PACK))
            for quarter in range(scalar_quarters, 4, 2):
                deal(on_vector, line_bf[c, a], line_raw[c, a], quarter, min(2, 4 - quarter), slice(0, PACK))

        def quantise(words, plane, values):
            nc.vector.quantize_mx(out=words.bitcast(FP8X4), scales=plane, in_=values)

        def quantise_line(c, a):
            line_q[c, a] = (kept([P, PASS], U32, "line_words%d%d" % (c, a)), kept([P, PASS], U8, "line_sc%d%d" % (c, a)))
            quantise(line_q[c, a][0][:], line_q[c, a][1][:], line_bf[c, a][:].rearrange("p t m i -> p (t m i)"))

        def quantise_lines(c):
            words, plane = kept([P, PASSES, PASS], U32, "line_words1"), kept([P, PASSES, PASS], U8, "line_sc1")
            quantise(words[:].rearrange("p a m -> p (a m)"), plane[:].rearrange("p a m -> p (a m)"), line_bf1[:].rearrange("p a t m i -> p (a t m i)"))
            for a in range(PASSES):
                line_q[c, a] = (words[:, a, :], plane[:, a, :])

        def quantise_state(c, first, last):
            ms = slice(P * first, P * (last + 1))
            quantise(state_words[c][:, ms], state_sc[c][:, ms], state_bf[c][:, first : last + 1].rearrange("p t m i -> p (t m i)"))

        def by_slot(bank):
            return bank[:].rearrange("j (m t) -> j t m", t=PACK)

        def by_group(bank):
            return bank[:].rearrange("p (t j) -> p t j", t=PACK)

        def by_two(bank):
            return bank[:].rearrange("p (t g e) -> p g t e", t=PACK, e=2)

        def adjacent(c, jt, bank, passes=(0, 1)):
            js = slice(P * jt, P * (jt + 1))
            adj = banks[bank]
            for a in passes:
                nc.tensor.matmul_mx(
                    out=adj[:], lhsT=picked["adj", a][:, js].bitcast(FP8X4), lhsT_scale=(picked_sc, shifted)[a]["adj"][:, js],
                    rhs=adj_w[c][:, a, :].bitcast(FP8X4), rhs_scale=adj_sc[:, a, PASS * c : PASS * (c + 1)],
                    start=(a == 0), stop=(a == PASSES - 1),
                )
            if passes[-1] == 0:
                return
            adj_sb[c, jt] = kept([P, PACK, P], F32, "adj_sb%d%d" % (c, jt))
            nc.scalar.copy(out=adj_sb[c, jt][:], in_=by_slot(adj))

        def difference(c, jt, bank, passes=(0, 1)):
            js = slice(P * jt, P * (jt + 1))
            bus = banks[bank]
            for a in passes:
                nc.tensor.matmul_mx(
                    out=bus[:], lhsT=picked["bus", a][:, js].bitcast(FP8X4),
                    lhsT_scale=(picked_sc, shifted)[a]["bus"][:, js],
                    rhs=bus_w[c][:, a, :].bitcast(FP4X4), rhs_scale=bus_sc[:, a, PASS * c : PASS * (c + 1)],
                    start=(a == 0), stop=(a == PASSES - 1),
                )
            if passes[-1] == 0:
                return
            diffs[c, jt] = kept([P, PACK, P], F32, "diff%d%d" % (c, jt))
            nc.vector.tensor_tensor(out=diffs[c, jt][:], in0=by_slot(bus), in1=adj_sb[c, jt][:], op=ALU.subtract)

        def sine(c, jt, bank):
            turned = banks[bank]
            for t in range(PACK):
                nc.tensor.transpose(by_group(turned)[:, t, :], diffs[c, jt][:, t, :], ident[:])
            if (c, jt) in LATE_SINES:
                sines[c, jt] = state_raw[1][:, jt, :].rearrange("p (g t e) -> p g t e", t=PACK, e=2)
            else:
                sines[c, jt] = kept([P, P // 2, PACK, 2], F32, "sine%d%d" % (c, jt))[:]
            nc.scalar.activation(out=sines[c, jt], in_=by_two(turned), func=ACT.Sin)

        def h_rounded(c, first, last):
            if c == 1 and first >= 2:
                return state_raw[1][:, first, N // 2 :].bitcast(BF16).rearrange("p (j t) -> p j t", t=PACK)
            home = h_late[:] if c else last_piece[:, : S * PACK // 2].bitcast(BF16).rearrange("p (j t) -> p j t", t=PACK)
            return home[:, P * first : P * (last + 1), :]

        def line_pass(c, jt, bank, t, a, start, stop):
            js, ms = slice(P * jt, P * (jt + 1)), slice(P * t, P * (t + 1))
            words, plane = line_q[c, a]
            nc.tensor.matmul_mx(
                out=by_group(banks[bank])[:, t, :], lhsT=words[:, ms].bitcast(FP8X4), lhsT_scale=plane[:, ms],
                rhs=picked["line", a][:, js].bitcast(FP8X4), rhs_scale=(picked_sc, shifted)[a]["line"][:, js],
                start=start, stop=stop,
            )

        def open_line(c, jt, bank):
            for t in range(PACK):
                line_pass(c, jt, bank, t, 0, t == 0, False)

        def features(c, jt, bank, opened=False):
            line = banks[bank]
            for t in range(PACK):
                if opened:
                    line_pass(c, jt, bank, t, 1, False, t == PACK - 1)
                else:
                    for a in (1, 0):
                        line_pass(c, jt, bank, t, a, a == 1, a == 0)
            nc.vector.tensor_tensor(
                out=h_rounded(c, jt, jt).rearrange("p (g e) t -> p g t e", e=2), in0=by_two(line), in1=sines[c, jt], op=ALU.mult,
            )

        def sums(c, jt, adj_bank, bus_bank):
            adjacent(c, jt, adj_bank)
            adjacent(c, jt + 1, adj_bank + 1)
            difference(c, jt, bus_bank)
            difference(c, jt + 1, bus_bank + 1)

        def sines_of(c, jt, bank):
            sine(c, jt, bank)
            sine(c, jt + 1, bank + 1)

        def features_of(c, jt, bank):
            features(c, jt, bank)
            features(c, jt + 1, bank + 1)

        def round_state(c, scalar_quarters):
            for quarter in range(scalar_quarters):
                deal(on_scalar, state_bf[c], state_raw[c], quarter, 1, slice(0, PACK))
            for quarter in range(scalar_quarters, 4, 2):
                deal(on_vector, state_bf[c], state_raw[c], quarter, min(2, 4 - quarter), slice(0, PACK))

        def quantise_h(c, first, last):
            js = slice(P * first, P * (last + 1))
            quantise(h_words[c][:, js], h_sc[c][:, js], h_rounded(c, first, last).rearrange("p j t -> p (j t)"))

        def flow(c, t):
            ms = slice(P * t, P * (t + 1))
            nc.tensor.matmul_mx(
                out=banks[t][:], lhsT=state_words[c][:, ms].bitcast(FP8X4), lhsT_scale=state_sc[c][:, ms],
                rhs=h_words[c][:].bitcast(FP8X4), rhs_scale=h_sc[c][:],
                start=(c == 0), stop=(c == PASSES - 1),
            )

        def project(t):
            ts = slice(t, t + 1)
            if t % 2 == 0:
                nc.scalar.activation(out=y[:, t, :], in_=banks[t][:], func=ACT.Identity, bias=pin_inv[:, ts], scale=neg_inv[:, ts])
            else:
                nc.vector.tensor_scalar(
                    out=y[:, t, :], in0=banks[t][:], scalar1=neg_inv[:, ts], scalar2=pin_inv[:, ts], op0=ALU.mult, op1=ALU.add,
                )
            nc.sync.dma_start(out=out_0.rearrange("(p t) j -> p t j", t=PACK)[:, t, :], in_=y[:, t, :])

        def flow_part(c, first, last, bank):
            js = slice(P * first, P * (last + 1))
            width = js.stop - js.start
            for t in range(PACK):
                ms = slice(P * t, P * (t + 1))
                nc.tensor.matmul_mx(
                    out=banks[bank + t // 2][:, width * (t % 2) : width * (t % 2 + 1)],
                    lhsT=state_words[c][:, ms].bitcast(FP8X4), lhsT_scale=state_sc[c][:, ms],
                    rhs=h_words[c][:, js].bitcast(FP8X4), rhs_scale=h_sc[c][:, js],
                    start=(c == 0 and t % 2 == 0), stop=(c == PASSES - 1 and t % 2 == 1),
                )

        def project_part(first, last, bank, pair, on_scalar_engine):
            js = slice(P * first, P * (last + 1))
            width = js.stop - js.start
            for t in (2 * pair, 2 * pair + 1):
                ts = slice(t, t + 1)
                src = banks[bank + pair][:, width * (t % 2) : width * (t % 2 + 1)]
                if on_scalar_engine:
                    nc.scalar.activation(out=y[:, t, js], in_=src, func=ACT.Identity, bias=pin_inv[:, ts], scale=neg_inv[:, ts])
                else:
                    nc.vector.tensor_scalar(
                        out=y[:, t, js], in0=src, scalar1=neg_inv[:, ts], scalar2=pin_inv[:, ts], op0=ALU.mult, op1=ALU.add,
                    )

        def store_y(first, last, slots):
            js = slice(P * first, P * (last + 1))
            nc.sync.dma_start(out=out_0.rearrange("(p t) j -> p t j", t=PACK)[:, slots, js], in_=y[:, slots, js])

        def round_y(copy, first, end):
            gs = slice(first // RUN, end // RUN)
            copy(
                out=y_bf[:].rearrange("p (g e) t -> p g t e", e=RUN)[:, gs],
                in_=y[:].rearrange("p t (g e) -> p g t e", e=RUN)[:, gs],
            )

        def planes(first, last, queue):
            js = slice(P * first, P * (last + 1))
            quantise(y_words[:, js], y_sc[:, js], y_bf[:, js, :].rearrange("p j t -> p (j t)"))
            words_out = out_1[0].rearrange("p j t -> p (j t)").bitcast(I32)
            queue.dma_start(out=words_out[:, js], in_=y_words[:, js].bitcast(I32))

        nc.gpsimd.memset(tab_sc[:].bitcast(I32), 0)
        nc.vector.memset(bus_sc[:].bitcast(I32), 0)
        nc.vector.memset(adj_sc[:].bitcast(I32), 0)
        nc.vector.memset(sums_sc1[:].bitcast(I32), 0)
        nc.vector.memset(line_sc1[:].bitcast(I32), 0)
        load_list("adj", offs2)
        load_list("bus", offs)
        load_table_scales(nc.sync)
        make_identity(nc, ident[:])
        nc.vector.memset(warm[:, 0:1], 0.0)
        nc.scalar.activation(out=warm[:, 1:2], in_=warm[:, 0:1], func=ACT.Sin)
        load_table(0)
        load_adj(0)
        load_weight_scales(nc.sync, adj_sc, wadj_scales)
        load_list("line", offs3)
        load_table(1)
        gather_scales("bus")
        gather_scales("adj")
        shift_plane(nc.sync, sums_sc1, sums_sc)
        load_weight_scales(nc.sync, bus_sc, wbus_scales)
        load_bus(0)
        load_adj(1)
        load_bus(1)
        load_line(0, 0)
        gather_scales("line")
        shift_plane(nc.sync, line_sc1, picked_sc["line"])
        load_line(0, 1)
        load_line(1, 0)
        load_line(1, 1)
        load_state(0)
        load_state(1)
        load_constants(nc.sync)
        gather_words("adj", 0, 0, TILES - 1)
        gather_words("bus", 0, 0, TILES - 1)
        gather_words("adj", 1, 0, 1)
        gather_words("adj", 1, 2, 3)
        gather_words("bus", 1, 0, 1)
        gather_words("bus", 1, 2, 3)
        for jt in range(4):
            adjacent(0, jt, jt, (0,))
        for jt in range(4):
            adjacent(0, jt, jt, (1,))
        gather_words("line", 0, 0, TILES - 1)
        for jt in range(4):
            difference(0, jt, 4 + jt)
        gather_words("line", 1, 0, TILES - 1)
        adjacent(1, 0, 0)
        adjacent(1, 1, 1)
        sines_of(0, 0, 2)
        difference(1, 0, 4)
        difference(1, 1, 5)
        round_line(0, 0, 2)
        sines_of(0, 2, 0)
        quantise_line(0, 0)
        round_line(0, 1, 0)
        quantise_line(0, 1)
        adjacent(1, 2, 6)
        adjacent(1, 3, 7)
        difference(1, 2, 2)
        difference(1, 3, 3)
        round_line(1, 0, 4)
        sines_of(1, 0, 4)
        open_line(0, 0, 6)
        open_line(0, 1, 7)
        round_line(1, 1, 0)
        quantise_lines(1)
        features(0, 0, 6, True)
        features(0, 1, 7, True)
        sines_of(1, 2, 0)
        features(0, 2, 2)
        features(0, 3, 6)
        round_state(0, 4)
        quantise_h(0, 0, 3)
        quantise_state(0, 0, 3)
        features_of(1, 0, 4)
        round_state(1, 3)
        constants()
        quantise_h(1, 0, 1)
        quantise_state(1, 0, 3)
        flow_part(0, 0, 1, 2)
        flow_part(0, 2, 2, 6)
        flow_part(1, 0, 1, 2)
        features_of(1, 2, 4)
        flow_part(0, 3, 3, 0)
        project_part(0, 1, 2, 0, True)
        store_y(0, 1, slice(0, 2))
        project_part(0, 1, 2, 1, True)
        store_y(0, 1, slice(2, 4))
        quantise_h(1, 2, 2)
        flow_part(1, 2, 2, 6)
        quantise_h(1, 3, 3)
        flow_part(1, 3, 3, 0)
        project_part(2, 2, 6, 1, False)
        project_part(3, 3, 0, 1, False)
        project_part(2, 2, 6, 0, True)
        project_part(3, 3, 0, 0, True)
        store_y(2, 3, slice(0, 4))
        round_y(on_scalar, 0, 128)
        round_y(on_vector, 128, 256)
        round_y(on_vector, 256, 432)
        round_y(on_scalar, 432, 512)
        planes(0, 1, nc.scalar)
        planes(2, 3, nc.scalar)
        for q in range(QUADS):
            queue = nc.scalar if q % 2 else nc.sync
            queue.dma_start(out=out_2[0, 4 * q : 4 * q + 4, :].bitcast(I32), in_=y_sc[32 * q : 32 * q + 4, :].bitcast(I32))
